import numpy as np
import ml_dtypes


def mxq(x, axis, fmt="e4m3"):
    dtype, down = {"e4m3": (ml_dtypes.float8_e4m3fn, 7), "e5m2": (ml_dtypes.float8_e5m2, 14)}[fmt]
    v = np.moveaxis(np.asarray(x, np.float32).astype(ml_dtypes.bfloat16).astype(np.float64), axis, -1)
    blocks = v.reshape(v.shape[:-1] + (-1, 32))
    amax = np.abs(blocks).max(-1, keepdims=True)
    byte = np.maximum(np.where(amax > 0, np.frexp(amax)[1] - 1 + 127, 0) - down, 1)
    scale = np.exp2(byte - 127.0)
    codes = (blocks / scale).astype(np.float32).astype(dtype).astype(np.float64)
    return np.moveaxis((codes * scale).reshape(v.shape), -1, axis)


WIDE = False


def mx_kscale(k):
    if not WIDE:
        return np.ones(k)
    levels = np.array([10, -10, 5, -5, 0])
    if k % 512:
        return np.exp2(np.random.permutation(np.resize(levels, k // 32))).repeat(32)
    a = np.empty((k // 512, 16))
    for p in range(k // 512):
        a[p, :8] = np.random.permutation(np.resize(levels, 8))
        for g in range(8):
            far = levels[np.abs(levels - a[p, g]) >= 10]
            a[p, g + 8] = far[np.random.randint(len(far))]
    return np.exp2(a.ravel()).repeat(32)


def f64(x):
    return np.asarray(x).astype(np.float64)


def striped(idx):
    return np.tile(idx.reshape(-1, 16).T, (8, 1)).astype(np.uint16)


def unstriped(offs):
    return offs[:16].T.reshape(-1).astype(np.int64)


E2M1 = np.array([0.0, 0.5, 1.0, 1.5, 2.0, 3.0, 4.0, 6.0, -0.0, -0.5, -1.0, -1.5, -2.0, -3.0, -4.0, -6.0])


def pack_weight(w, fmt):
    k, n = w.shape
    w = f64(np.asarray(w, np.float32).astype(ml_dtypes.bfloat16)).reshape(k // 32, 32, n)
    amax = np.abs(w).max(1)
    if fmt == "e4m3":
        byte = np.frexp(amax)[1] - 1 + 127 - 7
    else:
        mant, ex = np.frexp(amax / 6.0)
        byte = np.where(mant > 0.5, ex, ex - 1) + 127
    byte = np.clip(np.where(amax > 0, byte, 1), 1, 254)
    scaled = (w * np.exp2(127.0 - byte)[:, None, :]).reshape(k, n).astype(np.float32)
    by_word = np.ascontiguousarray(scaled.reshape(k // 512, 128, 4, n).transpose(0, 1, 3, 2))
    if fmt == "e4m3":
        words = by_word.astype(ml_dtypes.float8_e4m3fn).view(np.uint8)
    else:
        c = by_word.astype(ml_dtypes.float4_e2m1fn).view(np.uint8) & 0xF
        words = (c[..., 0::2] | (c[..., 1::2] << 4)).reshape(k // 512, 128, 2 * n)
    return np.ascontiguousarray(words), np.ascontiguousarray(byte.astype(np.uint8).reshape(k // 512, 16, n))


def unpack_weight(words, scales, fmt):
    g, _, n = scales.shape
    words = np.ascontiguousarray(words).reshape(g, 128, n, -1)
    if fmt == "e4m3":
        vals = words.view(ml_dtypes.float8_e4m3fn).astype(np.float64)
    else:
        nib = np.empty((g, 128, n, 4), np.uint8)
        nib[..., 0::2] = words & 0xF
        nib[..., 1::2] = words >> 4
        vals = E2M1[nib]
    vals = vals * np.repeat(np.exp2(scales.astype(np.float64) - 127.0), 8, axis=1)[..., None]
    return vals.transpose(0, 1, 3, 2).reshape(g * 512, n)


def gelu(v):
    return 0.5 * v * (1.0 + np.tanh(np.sqrt(2.0 / np.pi) * (v + 0.044715 * v**3)))


T, S, P, K, H = 4096, 1024, 512, 1536, 1024

def setup_inputs():
    n = np.random.standard_normal
    s = mx_kscale(K)[:, None]
    u = mx_kscale(H)[:, None]
    tab_words, tab_scales = pack_weight(n((K, T)) * s, "e4m3")
    w2_words, w2_scales = pack_weight(1.5 * n((H, H)) / np.sqrt(H) / u, "e2m1")
    return {
        "tab_words": tab_words,
        "tab_scales": tab_scales,
        "offs": striped(np.random.permutation(T)[:S]),
        "pos1": striped(np.random.permutation(S)[:P]),
        "pos2": striped(np.random.permutation(S)[:P]),
        "w1": (n((K, H)) / np.sqrt(K) / s).astype(np.float32),
        "w2_words": w2_words,
        "w2_scales": w2_scales,
        "gn": (np.exp(0.3 * n(H)) * u[:, 0]).astype(np.float32),
        "rs": np.exp(0.3 * n(H)).astype(np.float32),
    }

def reference(tab_words, tab_scales, offs, pos1, pos2, w1, w2_words, w2_scales, gn, rs):
    v = unpack_weight(tab_words, tab_scales, "e4m3")[:, unstriped(offs)]
    h = mxq(f64(w1), 0, "e4m3").T @ v
    x = np.tanh(h[:, unstriped(pos1)]) * f64(gn)[:, None]
    w2 = unpack_weight(w2_words, w2_scales, "e2m1")
    y = w2.T @ mxq(x, 0, "e4m3")
    z = y + f64(rs)[:, None] * h[:, unstriped(pos2)]
    return z / (1.0 + np.exp(-z)) + z

@@ -1,0 +1,217 @@
+from contextlib import ExitStack
+
+import concourse.mybir as mybir
+
+T, S, M, K, H = 4096, 1024, 512, 1536, 1024
+FLOPS = 2 * K * H * S + 2 * H * H * M
+
+F32 = mybir.dt.float32
+BF16 = mybir.dt.bfloat16
+I32 = mybir.dt.int32
+U32 = mybir.dt.uint32
+U16 = mybir.dt.uint16
+U8 = mybir.dt.uint8
+FP8X4 = mybir.dt.float8_e4m3fn_x4
+FP4X4 = mybir.dt.float4_e2m1fn_x4
+ACT = mybir.ActivationFunctionType
+ALU = mybir.AluOpType
+
+P = 128
+PACK = 4
+PASS = P * PACK
+K_PASSES = K // PASS
+H_PASSES = H // PASS
+BANK = 512
+QUADS = 4
+VEC_SHARE = {(0, 0): 0, (1, 0): 0, (2, 0): 84, (0, 1): 128, (1, 1): 0, (2, 1): 32}
+
+
+def tile_list_fiddle_phrase_variation_kernel(
+    tc, tab_words, tab_scales, offs, pos1, pos2, w1, w2_words, w2_scales, gn, rs, out
+):
+    nc = tc.nc
+    with ExitStack() as ctx:
+        keep = ctx.enter_context(tc.tile_pool(name="keep", bufs=1))
+        ring = ctx.enter_context(tc.tile_pool(name="ring", bufs=2))
+        psum = ctx.enter_context(tc.psum_pool(name="psum", bufs=1))
+
+        offs_sb = keep.tile([P, S // 16], U16, name="offs_sb")
+        pos1_sb = keep.tile([P, M // 16], U16, name="pos1_sb")
+        pos2_sb = keep.tile([P, M // 16], U16, name="pos2_sb")
+        tab_w = [keep.tile([P, T], I32, name=f"tab_w{a}") for a in range(K_PASSES)]
+        tab_s = keep.tile([P, T], U8, name="tab_s")
+        w2_w = keep.tile([P, H_PASSES * H * 2], U8, name="w2_w")
+        w2_s = keep.tile([P, H_PASSES * H], U8, name="w2_s")
+        gn_sb = keep.tile([P, H_PASSES, PACK], F32, name="gn_sb")
+        rs_sb = keep.tile([P, H_PASSES, PACK], F32, name="rs_sb")
+
+        nc.vector.memset(tab_s[:].bitcast(I32), 0)
+        nc.vector.memset(w2_s[:].bitcast(I32), 0)
+        def load_table(a):
+            nc.sync.dma_start(out=tab_w[a][:], in_=tab_words[a].rearrange("p t i -> p (t i)").bitcast(I32))
+
+        w1_raw = {}
+
+        def load_w1(a, b):
+            w1_raw[a, b] = ring.tile([P, PACK, PASS], F32, name="w1_raw", bufs=4)
+            rows = w1[a * PASS : (a + 1) * PASS, b * PASS : (b + 1) * PASS]
+            nc.sync.dma_start(out=w1_raw[a, b][:], in_=rows.rearrange("(p j) c -> p j c", j=PACK))
+
+        load_table(0)
+        for q in range(QUADS):
+            nc.sync.dma_start(
+                out=tab_s[32 * q : 32 * q + 4 * K_PASSES, :].bitcast(I32),
+                in_=tab_scales[:, 4 * q : 4 * q + 4, :].bitcast(I32),
+            )
+        nc.sync.dma_start(offs_sb[:], offs)
+        load_w1(0, 0)
+        load_table(1)
+        load_w1(1, 0)
+        for q in range(QUADS):
+            nc.sync.dma_start(
+                out=w2_s[32 * q : 32 * q + 4, :].bitcast(I32).rearrange("r (a c) -> r a c", a=H_PASSES),
+                in_=w2_scales[:, 4 * q : 4 * q + 4, :].bitcast(I32).rearrange("a r c -> r a c"),
+            )
+        load_table(2)
+        nc.sync.dma_start(pos1_sb[:], pos1)
+        nc.sync.dma_start(out=gn_sb[:], in_=gn.rearrange("(b p t) -> p b t", p=P, t=PACK))
+        load_w1(2, 0)
+        nc.sync.dma_start(
+            out=w2_w[:].bitcast(I32).rearrange("p (a c) -> p a c", a=H_PASSES),
+            in_=w2_words.bitcast(I32).rearrange("a p c -> p a c"),
+        )
+        load_w1(0, 1)
+        nc.sync.dma_start(out=rs_sb[:], in_=rs.rearrange("(b p t) -> p b t", p=P, t=PACK))
+        nc.sync.dma_start(pos2_sb[:], pos2)
+        load_w1(1, 1)
+        load_w1(2, 1)
+
+        v_w = [keep.tile([P, S], U32, name=f"v_w{a}", align_bytes=64) for a in range(K_PASSES)]
+        v_s = keep.tile([P, S], U8, name="v_s", align_bytes=64)
+
+        def gather_table(a):
+            for half in range(2):
+                nc.vector.tensor_copy(
+                    v_w[a][:, half * BANK : (half + 1) * BANK],
+                    tab_w[a][:].bitcast(U32).indirect(offs_sb[:, half * 32 : (half + 1) * 32]),
+                )
+
+        banks = {}
+
+        w1_q = {}
+
+        def quantise_w1(a, b):
+            grouped = ring.tile([P, PACK * PASS], BF16, name="w1_grouped", align_bytes=64)
+            src = w1_raw[a, b][:].rearrange("p j (m t) -> p m t j", t=PACK)
+            dst = grouped[:].rearrange("p (t m j) -> p m t j", t=PACK, j=PACK)
+            cut = P - VEC_SHARE[a, b]
+            if cut > 0:
+                nc.scalar.copy(dst[:, :cut], src[:, :cut])
+            if cut < P:
+                nc.vector.tensor_copy(dst[:, cut:], src[:, cut:])
+            codes = ring.tile([P, PASS], U32, name="w1_codes", align_bytes=64, bufs=3)
+            scales = ring.tile([P, PASS], U8, name="w1_scales", align_bytes=64, bufs=3)
+            nc.vector.quantize_mx(out=codes[:].bitcast(FP8X4), scales=scales[:], in_=grouped[:])
+            w1_q[a, b] = (codes, scales)
+
+        def first_product(a, b, t):
+            codes, scales = w1_q[a, b]
+            for half in range(2):
+                if a == 0:
+                    banks[b, t, half] = psum.tile([P, BANK], F32, name=f"bank{2 * t + half}")
+                cols = slice(half * BANK, (half + 1) * BANK)
+                nc.tensor.matmul_mx(
+                    out=banks[b, t, half][:],
+                    lhsT=codes[:, t * P : (t + 1) * P].bitcast(FP8X4),
+                    lhsT_scale=scales[:, t * P : (t + 1) * P],
+                    rhs=v_w[a][:, cols].bitcast(FP8X4),
+                    rhs_scale=v_s[4 * a :, cols],
+                    start=(a == 0),
+                    stop=(a == K_PASSES - 1),
+                )
+
+        def first_products(b):
+            for t in range(PACK):
+                first_product(0, b, t)
+            for t in range(PACK):
+                for a in range(1, K_PASSES):
+                    first_product(a, b, t)
+
+        h = {}
+        parents = {}
+
+        def fetch_parents(b, t):
+            h[b, t] = keep.tile([P, S], F32, name=f"h{b}{t}")
+            for half in range(2):
+                nc.scalar.copy(h[b, t][:, half * BANK : (half + 1) * BANK], banks[b, t, half][:])
+            parents[b, t] = ring.tile([P, M], F32, name="parents", bufs=8)
+            nc.vector.tensor_copy(parents[b, t][:], h[b, t][:].indirect(pos1_sb[:]))
+
+        x_codes = [keep.tile([P, M], U32, name=f"x_codes{b}", align_bytes=64) for b in range(H_PASSES)]
+        x_scales = [keep.tile([P, M], U8, name=f"x_scales{b}", align_bytes=64) for b in range(H_PASSES)]
+
+        def quantise_x(b):
+            planes = ring.tile([P, PACK, M], BF16, name="x_planes", bufs=2)
+            for t in range(PACK):
+                squashed = ring.tile([P, M], F32, name="squashed")
+                nc.scalar.activation(squashed[:], parents[b, t][:], ACT.Tanh)
+                nc.scalar.activation(planes[:, t, :], squashed[:], ACT.Copy, scale=gn_sb[:, b, t : t + 1])
+            grouped = ring.tile([P, M * PACK], BF16, name="x_grouped", align_bytes=64, bufs=1)
+            nc.vector.tensor_copy(
+                grouped[:].rearrange("p (c i t) -> p c t i", i=4, t=PACK),
+                planes[:].rearrange("p t (c i) -> p c t i", i=4),
+            )
+            nc.vector.quantize_mx(out=x_codes[b][:].bitcast(FP8X4), scales=x_scales[b][:], in_=grouped[:])
+
+        gather_table(0)
+        nc.vector.tensor_copy(v_s[:], tab_s[:].indirect(offs_sb[:]))
+        quantise_w1(0, 0)
+        w2p_s = keep.tile([P, H_PASSES * H], U8, name="w2p_s", align_bytes=64)
+        nc.vector.tensor_copy(
+            w2p_s[:].rearrange("p (g t u v) -> p g u t v", t=PACK, u=8, v=16),
+            w2_s[:].rearrange("p (g u v t) -> p g u t v", t=PACK, u=8, v=16),
+        )
+        for a in range(1, K_PASSES):
+            gather_table(a)
+            quantise_w1(a, 0)
+        w2p_w = keep.tile([P, H_PASSES * H * 2], U8, name="w2p_w", align_bytes=64)
+        nc.vector.tensor_copy(
+            w2p_w[:].bitcast(U16).rearrange("p (g t u v) -> p g u t v", t=PACK, u=16, v=8),
+            w2_w[:].bitcast(U16).rearrange("p (g u v t) -> p g u t v", t=PACK, u=16, v=8),
+        )
+        first_products(0)
+        for t in range(PACK):
+            fetch_parents(0, t)
+        for a in range(K_PASSES):
+            quantise_w1(a, 1)
+        first_products(1)
+        for t in range(PACK):
+            fetch_parents(1, t)
+        quantise_x(0)
+        quantise_x(1)
+        skip_room = [w1_raw[2, 1][:, 0, :], w1_raw[2, 1][:, 1, :], parents[1, 0][:], parents[1, 1][:]]
+
+        out_rows = out.rearrange("(b p t) m -> b t p m", p=P, t=PACK)
+        for b in range(H_PASSES):
+            for t in range(PACK):
+                skip = skip_room[t]
+                nc.vector.tensor_copy(skip, h[b, t][:].indirect(pos2_sb[:]))
+                y = psum.tile([P, BANK], F32, name=f"bank{PACK * b + t}")
+                for a in range(H_PASSES):
+                    col = a * H + b * PASS + t * P
+                    nc.tensor.matmul_mx(
+                        out=y[:],
+                        lhsT=w2p_w[:, 2 * col : 2 * (col + P)].bitcast(FP4X4),
+                        lhsT_scale=w2p_s[:, col : col + P],
+                        rhs=x_codes[a][:].bitcast(FP8X4),
+                        rhs_scale=x_scales[a][:],
+                        start=(a == 0),
+                        stop=(a == H_PASSES - 1),
+                    )
+                z = ring.tile([P, M], F32, name="z", bufs=3)
+                nc.vector.scalar_tensor_tensor(z[:], skip, rs_sb[:, b, t : t + 1], y[:], ALU.mult, ALU.add)
+                gated = ring.tile([P, M], F32, name="gated", bufs=3)
+                nc.scalar.activation(gated[:], z[:], ACT.Silu)
+                res = ring.tile([P, M], F32, name="res", bufs=3)
+                nc.vector.tensor_tensor(res[:], gated[:], z[:], ALU.add)
+                nc.sync.dma_start(out=out_rows[b, t], in_=res[:])

@@ -213,5 +213,5 @@ def tile_list_fiddle_phrase_variation_kernel(
                 gated = ring.tile([P, M], F32, name="gated", bufs=3)
                 nc.scalar.activation(gated[:], z[:], ACT.Silu)
                 res = ring.tile([P, M], F32, name="res", bufs=3)
-                nc.vector.tensor_tensor(res[:], gated[:], z[:], ALU.add)
+                nc.gpsimd.tensor_tensor(res[:], gated[:], z[:], ALU.add)
                 nc.sync.dma_start(out=out_rows[b, t], in_=res[:])

@@ -22,8 +22,15 @@ PASS = P * PACK
 K_PASSES = K // PASS
 H_PASSES = H // PASS
 BANK = 512
+HALVES = S // BANK
 QUADS = 4
-VEC_SHARE = {(0, 0): 0, (1, 0): 0, (2, 0): 84, (0, 1): 128, (1, 1): 0, (2, 1): 32}
+ROWS = 4
+PER_COLUMN = 16
+LAST_SLICE = (H_PASSES - 1, PACK - 1)
+
+VECTOR_COLUMNS = {(2, 0): 84, (0, 1): P}
+GPSIMD_PIECE = (1, 1)
+GPSIMD_SUMS = 6
 
 
 def tile_list_fiddle_phrase_variation_kernel(
@@ -35,9 +42,9 @@ def tile_list_fiddle_phrase_variation_kernel(
         ring = ctx.enter_context(tc.tile_pool(name="ring", bufs=2))
         psum = ctx.enter_context(tc.psum_pool(name="psum", bufs=1))
 
-        offs_sb = keep.tile([P, S // 16], U16, name="offs_sb")
-        pos1_sb = keep.tile([P, M // 16], U16, name="pos1_sb")
-        pos2_sb = keep.tile([P, M // 16], U16, name="pos2_sb")
+        offs_sb = keep.tile([P, S // PER_COLUMN], U16, name="offs_sb")
+        pos1_sb = keep.tile([P, M // PER_COLUMN], U16, name="pos1_sb")
+        pos2_sb = keep.tile([P, M // PER_COLUMN], U16, name="pos2_sb")
         tab_w = [keep.tile([P, T], I32, name=f"tab_w{a}") for a in range(K_PASSES)]
         tab_s = keep.tile([P, T], U8, name="tab_s")
         w2_w = keep.tile([P, H_PASSES * H * 2], U8, name="w2_w")
@@ -47,6 +54,7 @@ def tile_list_fiddle_phrase_variation_kernel(
 
         nc.vector.memset(tab_s[:].bitcast(I32), 0)
         nc.vector.memset(w2_s[:].bitcast(I32), 0)
+
         def load_table(a):
             nc.sync.dma_start(out=tab_w[a][:], in_=tab_words[a].rearrange("p t i -> p (t i)").bitcast(I32))
 
@@ -59,73 +67,84 @@ def tile_list_fiddle_phrase_variation_kernel(
 
         load_table(0)
         for q in range(QUADS):
-            nc.sync.dma_start(
-                out=tab_s[32 * q : 32 * q + 4 * K_PASSES, :].bitcast(I32),
-                in_=tab_scales[:, 4 * q : 4 * q + 4, :].bitcast(I32),
+            nc.gpsimd.dma_start(
+                out=tab_s[32 * q : 32 * q + ROWS * K_PASSES, :].bitcast(I32),
+                in_=tab_scales[:, ROWS * q : ROWS * (q + 1), :].bitcast(I32),
             )
         nc.sync.dma_start(offs_sb[:], offs)
         load_w1(0, 0)
         load_table(1)
         load_w1(1, 0)
         for q in range(QUADS):
-            nc.sync.dma_start(
-                out=w2_s[32 * q : 32 * q + 4, :].bitcast(I32).rearrange("r (a c) -> r a c", a=H_PASSES),
-                in_=w2_scales[:, 4 * q : 4 * q + 4, :].bitcast(I32).rearrange("a r c -> r a c"),
+            nc.gpsimd.dma_start(
+                out=w2_s[32 * q : 32 * q + ROWS, :].bitcast(I32).rearrange("r (a c) -> r a c", a=H_PASSES),
+                in_=w2_scales[:, ROWS * q : ROWS * (q + 1), :].bitcast(I32).rearrange("a r c -> r a c"),
             )
         load_table(2)
-        nc.sync.dma_start(pos1_sb[:], pos1)
-        nc.sync.dma_start(out=gn_sb[:], in_=gn.rearrange("(b p t) -> p b t", p=P, t=PACK))
         load_w1(2, 0)
         nc.sync.dma_start(
             out=w2_w[:].bitcast(I32).rearrange("p (a c) -> p a c", a=H_PASSES),
             in_=w2_words.bitcast(I32).rearrange("a p c -> p a c"),
         )
         load_w1(0, 1)
-        nc.sync.dma_start(out=rs_sb[:], in_=rs.rearrange("(b p t) -> p b t", p=P, t=PACK))
-        nc.sync.dma_start(pos2_sb[:], pos2)
+        nc.sync.dma_start(pos1_sb[:], pos1)
         load_w1(1, 1)
         load_w1(2, 1)
+        nc.sync.dma_start(pos2_sb[:], pos2)
+        nc.sync.dma_start(out=gn_sb[:], in_=gn.rearrange("(b p t) -> p b t", p=P, t=PACK))
+        nc.sync.dma_start(out=rs_sb[:], in_=rs.rearrange("(b p t) -> p b t", p=P, t=PACK))
 
         v_w = [keep.tile([P, S], U32, name=f"v_w{a}", align_bytes=64) for a in range(K_PASSES)]
         v_s = keep.tile([P, S], U8, name="v_s", align_bytes=64)
 
         def gather_table(a):
-            for half in range(2):
+            columns = BANK // PER_COLUMN
+            for half in range(HALVES):
                 nc.vector.tensor_copy(
                     v_w[a][:, half * BANK : (half + 1) * BANK],
-                    tab_w[a][:].bitcast(U32).indirect(offs_sb[:, half * 32 : (half + 1) * 32]),
+                    tab_w[a][:].bitcast(U32).indirect(offs_sb[:, half * columns : (half + 1) * columns]),
                 )
 
-        banks = {}
-
-        w1_q = {}
+        w1_grouped = {}
+        w1_quantised = {}
+        late_scales = keep.tile([P, PASS], U8, name="late_scales", align_bytes=64)
 
         def quantise_w1(a, b):
-            grouped = ring.tile([P, PACK * PASS], BF16, name="w1_grouped", align_bytes=64)
+            grouped = w1_grouped[a, b] = ring.tile([P, PACK * PASS], BF16, name="w1_grouped", align_bytes=64, bufs=3)
             src = w1_raw[a, b][:].rearrange("p j (m t) -> p m t j", t=PACK)
             dst = grouped[:].rearrange("p (t m j) -> p m t j", t=PACK, j=PACK)
-            cut = P - VEC_SHARE[a, b]
-            if cut > 0:
+            cut = P - VECTOR_COLUMNS.get((a, b), 0)
+            if (a, b) == GPSIMD_PIECE:
+                nc.gpsimd.tensor_scalar(dst, src, 1.0, 0.0, ALU.mult, ALU.add)
+            elif cut > 0:
                 nc.scalar.copy(dst[:, :cut], src[:, :cut])
             if cut < P:
                 nc.vector.tensor_copy(dst[:, cut:], src[:, cut:])
-            codes = ring.tile([P, PASS], U32, name="w1_codes", align_bytes=64, bufs=3)
-            scales = ring.tile([P, PASS], U8, name="w1_scales", align_bytes=64, bufs=3)
-            nc.vector.quantize_mx(out=codes[:].bitcast(FP8X4), scales=scales[:], in_=grouped[:])
-            w1_q[a, b] = (codes, scales)
+            if (a, b) == (K_PASSES - 1, H_PASSES - 1):
+                codes = keep.tile([P, PASS], U32, name="last_codes", tag="last_codes", align_bytes=64)
+            else:
+                codes = ring.tile([P, PASS], U32, name="w1_codes", align_bytes=64, bufs=3)
+            if b == H_PASSES - 1 and a > 0:
+                scales = late_scales[ROWS * a :, :]
+            else:
+                scales = ring.tile([P, PASS], U8, name="w1_scales", align_bytes=64, bufs=3)[:]
+            nc.vector.quantize_mx(out=codes[:].bitcast(FP8X4), scales=scales, in_=grouped[:])
+            w1_quantised[a, b] = (codes, scales)
+
+        banks = {}
 
         def first_product(a, b, t):
-            codes, scales = w1_q[a, b]
-            for half in range(2):
+            codes, scales = w1_quantised[a, b]
+            for half in range(HALVES):
                 if a == 0:
-                    banks[b, t, half] = psum.tile([P, BANK], F32, name=f"bank{2 * t + half}")
+                    banks[b, t, half] = psum.tile([P, BANK], F32, name=f"bank{HALVES * t + half}")
                 cols = slice(half * BANK, (half + 1) * BANK)
                 nc.tensor.matmul_mx(
                     out=banks[b, t, half][:],
                     lhsT=codes[:, t * P : (t + 1) * P].bitcast(FP8X4),
                     lhsT_scale=scales[:, t * P : (t + 1) * P],
                     rhs=v_w[a][:, cols].bitcast(FP8X4),
-                    rhs_scale=v_s[4 * a :, cols],
+                    rhs_scale=v_s[ROWS * a :, cols],
                     start=(a == 0),
                     stop=(a == K_PASSES - 1),
                 )
@@ -142,26 +161,48 @@ def tile_list_fiddle_phrase_variation_kernel(
 
         def fetch_parents(b, t):
             h[b, t] = keep.tile([P, S], F32, name=f"h{b}{t}")
-            for half in range(2):
+            for half in range(HALVES):
                 nc.scalar.copy(h[b, t][:, half * BANK : (half + 1) * BANK], banks[b, t, half][:])
-            parents[b, t] = ring.tile([P, M], F32, name="parents", bufs=8)
+            parents[b, t] = keep.tile([P, M], F32, name=f"parents{b}{t}", tag=f"parents{b}{t}", align_bytes=64)
             nc.vector.tensor_copy(parents[b, t][:], h[b, t][:].indirect(pos1_sb[:]))
 
-        x_codes = [keep.tile([P, M], U32, name=f"x_codes{b}", align_bytes=64) for b in range(H_PASSES)]
+        x_grouped = {}
+        x_codes = {}
         x_scales = [keep.tile([P, M], U8, name=f"x_scales{b}", align_bytes=64) for b in range(H_PASSES)]
 
-        def quantise_x(b):
-            planes = ring.tile([P, PACK, M], BF16, name="x_planes", bufs=2)
+        def make_x(b):
+            rounded = ring.tile([P, PACK, M], BF16, name="x_rounded", bufs=H_PASSES)
+            if b == 0:
+                squashed = w1_raw[K_PASSES - 1, H_PASSES - 1]
+            else:
+                squashed = keep.tile([P, PACK, M], F32, name="squashed", tag="last_codes", align_bytes=64)
             for t in range(PACK):
-                squashed = ring.tile([P, M], F32, name="squashed")
-                nc.scalar.activation(squashed[:], parents[b, t][:], ACT.Tanh)
-                nc.scalar.activation(planes[:, t, :], squashed[:], ACT.Copy, scale=gn_sb[:, b, t : t + 1])
-            grouped = ring.tile([P, M * PACK], BF16, name="x_grouped", align_bytes=64, bufs=1)
-            nc.vector.tensor_copy(
-                grouped[:].rearrange("p (c i t) -> p c t i", i=4, t=PACK),
-                planes[:].rearrange("p t (c i) -> p c t i", i=4),
+                nc.scalar.activation(squashed[:, t, :], parents[b, t][:], ACT.Tanh)
+                gain = gn_sb[:, b, t : t + 1]
+                if (b, t) == LAST_SLICE:
+                    nc.scalar.activation(rounded[:, t, :], squashed[:, t, :], ACT.Copy, scale=gain)
+                else:
+                    nc.gpsimd.tensor_scalar(rounded[:, t, :], squashed[:, t, :], gain, 0.0, ALU.mult, ALU.add)
+            grouped = x_grouped[b] = ring.tile([P, M * PACK], BF16, name="x_grouped", align_bytes=64, bufs=H_PASSES)
+            cut = M // 2 if b == H_PASSES - 1 else 0
+            if cut:
+                nc.scalar.copy(
+                    grouped[:, : PACK * cut].rearrange("p (c i t) -> p c t i", i=4, t=PACK),
+                    rounded[:, :, :cut].rearrange("p t (c i) -> p c t i", i=4),
+                )
+            nc.gpsimd.tensor_scalar(
+                grouped[:, PACK * cut :].rearrange("p (m t) -> p m t", t=PACK),
+                rounded[:, :, cut:].rearrange("p t m -> p m t"),
+                1.0,
+                0.0,
+                ALU.mult,
+                ALU.add,
             )
-            nc.vector.quantize_mx(out=x_codes[b][:].bitcast(FP8X4), scales=x_scales[b][:], in_=grouped[:])
+
+        def quantise_x(b):
+            tag = "parents10" if b == 0 else "x_codes1"
+            x_codes[b] = keep.tile([P, M], U32, name=f"x_codes{b}", tag=tag, align_bytes=64)
+            nc.vector.quantize_mx(out=x_codes[b][:].bitcast(FP8X4), scales=x_scales[b][:], in_=x_grouped[b][:])
 
         gather_table(0)
         nc.vector.tensor_copy(v_s[:], tab_s[:].indirect(offs_sb[:]))
@@ -180,23 +221,37 @@ def tile_list_fiddle_phrase_variation_kernel(
             w2_w[:].bitcast(U16).rearrange("p (g u v t) -> p g u t v", t=PACK, u=16, v=8),
         )
         first_products(0)
-        for t in range(PACK):
+        fetch_parents(0, 0)
+        quantise_w1(0, 1)
+        for t in range(1, PACK):
             fetch_parents(0, t)
-        for a in range(K_PASSES):
+        for a in range(1, K_PASSES):
             quantise_w1(a, 1)
         first_products(1)
         for t in range(PACK):
             fetch_parents(1, t)
-        quantise_x(0)
-        quantise_x(1)
-        skip_room = [w1_raw[2, 1][:, 0, :], w1_raw[2, 1][:, 1, :], parents[1, 0][:], parents[1, 1][:]]
+        for b in range(H_PASSES):
+            make_x(b)
+        for b in range(H_PASSES):
+            quantise_x(b)
+
+        skip_room = [
+            w1_grouped[1, 1][:].bitcast(F32)[:, :M],
+            w1_grouped[2, 1][:].bitcast(F32)[:, :M],
+            w1_grouped[2, 1][:].bitcast(F32)[:, M:],
+            parents[1, 1][:],
+            parents[1, 2][:],
+            x_grouped[1][:].bitcast(F32)[:, :M],
+        ]
+        skip_room = skip_room + skip_room[1:3]
 
         out_rows = out.rearrange("(b p t) m -> b t p m", p=P, t=PACK)
         for b in range(H_PASSES):
             for t in range(PACK):
-                skip = skip_room[t]
+                number = PACK * b + t
+                skip = skip_room[number]
                 nc.vector.tensor_copy(skip, h[b, t][:].indirect(pos2_sb[:]))
-                y = psum.tile([P, BANK], F32, name=f"bank{PACK * b + t}")
+                y = psum.tile([P, BANK], F32, name=f"bank{number}")
                 for a in range(H_PASSES):
                     col = a * H + b * PASS + t * P
                     nc.tensor.matmul_mx(
@@ -208,10 +263,17 @@ def tile_list_fiddle_phrase_variation_kernel(
                         start=(a == 0),
                         stop=(a == H_PASSES - 1),
                     )
-                z = ring.tile([P, M], F32, name="z", bufs=3)
-                nc.vector.scalar_tensor_tensor(z[:], skip, rs_sb[:, b, t : t + 1], y[:], ALU.mult, ALU.add)
-                gated = ring.tile([P, M], F32, name="gated", bufs=3)
-                nc.scalar.activation(gated[:], z[:], ACT.Silu)
-                res = ring.tile([P, M], F32, name="res", bufs=3)
-                nc.gpsimd.tensor_tensor(res[:], gated[:], z[:], ALU.add)
-                nc.sync.dma_start(out=out_rows[b, t], in_=res[:])
+                z = ring.tile([P, M], F32, name="z", bufs=4)
+                gated = ring.tile([P, M], F32, name="gated", bufs=4)
+                res = ring.tile([P, M], F32, name="res", bufs=6)
+                adder = nc.gpsimd if number < GPSIMD_SUMS else nc.vector
+                width = M // 2 if (b, t) == LAST_SLICE else M
+                parts = [slice(c, c + width) for c in range(0, M, width)]
+                for cols in parts:
+                    nc.vector.scalar_tensor_tensor(
+                        z[:, cols], skip[:, cols], rs_sb[:, b, t : t + 1], y[:, cols], ALU.mult, ALU.add
+                    )
+                    nc.scalar.activation(gated[:, cols], z[:, cols], ACT.Silu)
+                for cols in parts:
+                    adder.tensor_tensor(res[:, cols], gated[:, cols], z[:, cols], ALU.add)
+                    nc.sync.dma_start(out=out_rows[b, t][:, cols], in_=res[:, cols])

@@ -45,7 +45,7 @@ def tile_list_fiddle_phrase_variation_kernel(
         offs_sb = keep.tile([P, S // PER_COLUMN], U16, name="offs_sb")
         pos1_sb = keep.tile([P, M // PER_COLUMN], U16, name="pos1_sb")
         pos2_sb = keep.tile([P, M // PER_COLUMN], U16, name="pos2_sb")
-        tab_w = [keep.tile([P, T], I32, name=f"tab_w{a}") for a in range(K_PASSES)]
+        tab_w = [keep.tile([P, T], I32, name=f"tab_w{a}", tag=f"tab_w{a}") for a in range(K_PASSES)]
         tab_s = keep.tile([P, T], U8, name="tab_s")
         w2_w = keep.tile([P, H_PASSES * H * 2], U8, name="w2_w")
         w2_s = keep.tile([P, H_PASSES * H], U8, name="w2_s")
@@ -190,14 +190,19 @@ def tile_list_fiddle_phrase_variation_kernel(
                     grouped[:, : PACK * cut].rearrange("p (c i t) -> p c t i", i=4, t=PACK),
                     rounded[:, :, :cut].rearrange("p t (c i) -> p c t i", i=4),
                 )
-            nc.gpsimd.tensor_scalar(
-                grouped[:, PACK * cut :].rearrange("p (m t) -> p m t", t=PACK),
-                rounded[:, :, cut:].rearrange("p t m -> p m t"),
-                1.0,
-                0.0,
-                ALU.mult,
-                ALU.add,
-            )
+                nc.vector.tensor_copy(
+                    grouped[:, PACK * cut :].rearrange("p (c i t) -> p c t i", i=4, t=PACK),
+                    rounded[:, :, cut:].rearrange("p t (c i) -> p c t i", i=4),
+                )
+            else:
+                nc.gpsimd.tensor_scalar(
+                    grouped[:].rearrange("p (m t) -> p m t", t=PACK),
+                    rounded[:].rearrange("p t m -> p m t"),
+                    1.0,
+                    0.0,
+                    ALU.mult,
+                    ALU.add,
+                )
 
         def quantise_x(b):
             tag = "parents10" if b == 0 else "x_codes1"
@@ -240,11 +245,11 @@ def tile_list_fiddle_phrase_variation_kernel(
             w1_grouped[2, 1][:].bitcast(F32)[:, :M],
             w1_grouped[2, 1][:].bitcast(F32)[:, M:],
             parents[1, 1][:],
-            parents[1, 2][:],
             x_grouped[1][:].bitcast(F32)[:, :M],
         ]
-        skip_room = skip_room + skip_room[1:3]
+        skip_room = skip_room + skip_room[1:4]
 
+        rooms = [keep.tile([P, H // P, M], F32, name=f"room{a}", tag=f"tab_w{a}") for a in range(K_PASSES)]
         out_rows = out.rearrange("(b p t) m -> b t p m", p=P, t=PACK)
         for b in range(H_PASSES):
             for t in range(PACK):
@@ -263,9 +268,7 @@ def tile_list_fiddle_phrase_variation_kernel(
                         start=(a == 0),
                         stop=(a == H_PASSES - 1),
                     )
-                z = ring.tile([P, M], F32, name="z", bufs=4)
-                gated = ring.tile([P, M], F32, name="gated", bufs=4)
-                res = ring.tile([P, M], F32, name="res", bufs=6)
+                z, gated, res = (room[:, number, :] for room in rooms)
                 adder = nc.gpsimd if number < GPSIMD_SUMS else nc.vector
                 width = M // 2 if (b, t) == LAST_SLICE else M
                 parts = [slice(c, c + width) for c in range(0, M, width)]

@@ -1,6 +1,7 @@
 from contextlib import ExitStack
 
 import concourse.mybir as mybir
+from concourse.masks import make_identity
 
 T, S, M, K, H = 4096, 1024, 512, 1536, 1024
 FLOPS = 2 * K * H * S + 2 * H * H * M
@@ -26,11 +27,15 @@ HALVES = S // BANK
 QUADS = 4
 ROWS = 4
 PER_COLUMN = 16
-LAST_SLICE = (H_PASSES - 1, PACK - 1)
-
-VECTOR_COLUMNS = {(2, 0): 84, (0, 1): P}
-GPSIMD_PIECE = (1, 1)
+SLICES = H // P
+WIDE = 256
+GROUPS = H // WIDE
+PER_GROUP = WIDE // P
+PAIRS = [((1, 0), (1, 1)), ((1, 2), (2, 0)), ((2, 1), (2, 2)), ((3, 0), (3, 1)), (None, (3, 2))]
+UNIT = PACK * WIDE
 GPSIMD_SUMS = 6
+SCALAR_CUT = 176
+X0_SCALAR_CUT = 320
 
 
 def tile_list_fiddle_phrase_variation_kernel(
@@ -39,32 +44,37 @@ def tile_list_fiddle_phrase_variation_kernel(
     nc = tc.nc
     with ExitStack() as ctx:
         keep = ctx.enter_context(tc.tile_pool(name="keep", bufs=1))
-        ring = ctx.enter_context(tc.tile_pool(name="ring", bufs=2))
         psum = ctx.enter_context(tc.psum_pool(name="psum", bufs=1))
+
+        def tile(shape, dtype, name, tag=None):
+            return keep.tile(shape, dtype, name=name, tag=tag or name, align_bytes=64)
 
         offs_sb = keep.tile([P, S // PER_COLUMN], U16, name="offs_sb")
         pos1_sb = keep.tile([P, M // PER_COLUMN], U16, name="pos1_sb")
         pos2_sb = keep.tile([P, M // PER_COLUMN], U16, name="pos2_sb")
-        tab_w = [keep.tile([P, T], I32, name=f"tab_w{a}", tag=f"tab_w{a}") for a in range(K_PASSES)]
-        tab_s = keep.tile([P, T], U8, name="tab_s")
-        w2_w = keep.tile([P, H_PASSES * H * 2], U8, name="w2_w")
-        w2_s = keep.tile([P, H_PASSES * H], U8, name="w2_s")
-        gn_sb = keep.tile([P, H_PASSES, PACK], F32, name="gn_sb")
-        rs_sb = keep.tile([P, H_PASSES, PACK], F32, name="rs_sb")
+        tab_w = [tile([P, T], I32, f"tab_w{a}") for a in range(K_PASSES)]
+        tab_s = tile([P, T], U8, "tab_s")
+        w2_w = tile([P, H_PASSES * H * 2], U8, "w2_w")
+        w2_s = tile([P, H_PASSES * H], U8, "w2_s")
+        staged = tile([P, P], F32, "staged")
+        identity = tile([P, P], F32, "identity")
+        factors = tile([P, 2 * SLICES], F32, "factors")
 
         nc.vector.memset(tab_s[:].bitcast(I32), 0)
+        nc.vector.memset(staged[:], 0.0)
         nc.vector.memset(w2_s[:].bitcast(I32), 0)
 
         def load_table(a):
             nc.sync.dma_start(out=tab_w[a][:], in_=tab_words[a].rearrange("p t i -> p (t i)").bitcast(I32))
 
-        w1_raw = {}
+        raw = {}
 
-        def load_w1(a, b):
-            w1_raw[a, b] = ring.tile([P, PACK, PASS], F32, name="w1_raw", bufs=4)
-            rows = w1[a * PASS : (a + 1) * PASS, b * PASS : (b + 1) * PASS]
-            nc.sync.dma_start(out=w1_raw[a, b][:], in_=rows.rearrange("(p j) c -> p j c", j=PACK))
+        def load_w1(g, a):
+            raw[g, a] = tile([P, PACK, WIDE], F32, f"raw{g}{a}")
+            rows = w1[a * PASS : (a + 1) * PASS, g * WIDE : (g + 1) * WIDE]
+            nc.sync.dma_start(out=raw[g, a][:], in_=rows.rearrange("(p j) c -> p j c", j=PACK))
 
+        load_w1(0, 0)
         load_table(0)
         for q in range(QUADS):
             nc.gpsimd.dma_start(
@@ -72,30 +82,34 @@ def tile_list_fiddle_phrase_variation_kernel(
                 in_=tab_scales[:, ROWS * q : ROWS * (q + 1), :].bitcast(I32),
             )
         nc.sync.dma_start(offs_sb[:], offs)
-        load_w1(0, 0)
+        nc.sync.dma_start(pos1_sb[:], pos1)
+        nc.sync.dma_start(pos2_sb[:], pos2)
+        load_w1(0, 1)
+        load_w1(0, 2)
+        nc.sync.dma_start(out=staged[:SLICES, :], in_=gn.rearrange("(s p) -> s p", p=P))
+        nc.sync.dma_start(out=staged[SLICES : 2 * SLICES, :], in_=rs.rearrange("(s p) -> s p", p=P))
         load_table(1)
-        load_w1(1, 0)
-        for q in range(QUADS):
-            nc.gpsimd.dma_start(
-                out=w2_s[32 * q : 32 * q + ROWS, :].bitcast(I32).rearrange("r (a c) -> r a c", a=H_PASSES),
-                in_=w2_scales[:, ROWS * q : ROWS * (q + 1), :].bitcast(I32).rearrange("a r c -> r a c"),
-            )
         load_table(2)
-        load_w1(2, 0)
+        for g in range(1, GROUPS):
+            for a in range(K_PASSES):
+                load_w1(g, a)
         nc.sync.dma_start(
             out=w2_w[:].bitcast(I32).rearrange("p (a c) -> p a c", a=H_PASSES),
             in_=w2_words.bitcast(I32).rearrange("a p c -> p a c"),
         )
-        load_w1(0, 1)
-        nc.sync.dma_start(pos1_sb[:], pos1)
-        load_w1(1, 1)
-        load_w1(2, 1)
-        nc.sync.dma_start(pos2_sb[:], pos2)
-        nc.sync.dma_start(out=gn_sb[:], in_=gn.rearrange("(b p t) -> p b t", p=P, t=PACK))
-        nc.sync.dma_start(out=rs_sb[:], in_=rs.rearrange("(b p t) -> p b t", p=P, t=PACK))
+        for q in range(QUADS):
+            nc.sync.dma_start(
+                out=w2_s[32 * q : 32 * q + ROWS, :].bitcast(I32).rearrange("r (a c) -> r a c", a=H_PASSES),
+                in_=w2_scales[:, ROWS * q : ROWS * (q + 1), :].bitcast(I32).rearrange("a r c -> r a c"),
+            )
 
-        v_w = [keep.tile([P, S], U32, name=f"v_w{a}", align_bytes=64) for a in range(K_PASSES)]
-        v_s = keep.tile([P, S], U8, name="v_s", align_bytes=64)
+        make_identity(nc, identity[:])
+        turned = psum.tile([P, BANK], F32, name="bank7")
+        nc.tensor.transpose(turned[:, :P], staged[:], identity[:])
+        nc.scalar.copy(factors[:], turned[:, : 2 * SLICES])
+
+        v_w = [tile([P, S], U32, f"v_w{a}") for a in range(K_PASSES)]
+        v_s = tile([P, S], U8, "v_s")
 
         def gather_table(a):
             columns = BANK // PER_COLUMN
@@ -105,178 +119,215 @@ def tile_list_fiddle_phrase_variation_kernel(
                     tab_w[a][:].bitcast(U32).indirect(offs_sb[:, half * columns : (half + 1) * columns]),
                 )
 
-        w1_grouped = {}
-        w1_quantised = {}
-        late_scales = keep.tile([P, PASS], U8, name="late_scales", align_bytes=64)
+        quantised = {}
 
-        def quantise_w1(a, b):
-            grouped = w1_grouped[a, b] = ring.tile([P, PACK * PASS], BF16, name="w1_grouped", align_bytes=64, bufs=3)
-            src = w1_raw[a, b][:].rearrange("p j (m t) -> p m t j", t=PACK)
-            dst = grouped[:].rearrange("p (t m j) -> p m t j", t=PACK, j=PACK)
-            cut = P - VECTOR_COLUMNS.get((a, b), 0)
-            if (a, b) == GPSIMD_PIECE:
-                nc.gpsimd.tensor_scalar(dst, src, 1.0, 0.0, ALU.mult, ALU.add)
-            elif cut > 0:
-                nc.scalar.copy(dst[:, :cut], src[:, :cut])
-            if cut < P:
-                nc.vector.tensor_copy(dst[:, cut:], src[:, cut:])
-            if (a, b) == (K_PASSES - 1, H_PASSES - 1):
-                codes = keep.tile([P, PASS], U32, name="last_codes", tag="last_codes", align_bytes=64)
+        def round_on_scalar(piece, unit):
+            src = raw[piece][:].rearrange("p j (c i) -> p c j i", i=4)
+            nc.scalar.copy(unit.rearrange("p (c i j) -> p c j i", i=4, j=PACK), src)
+
+        def round_on_gpsimd(piece, unit):
+            src = raw[piece][:].rearrange("p j c -> p c j")
+            nc.gpsimd.tensor_scalar(unit.rearrange("p (c j) -> p c j", j=PACK), src, 1.0, 0.0, ALU.mult, ALU.add)
+
+        def quantise_w1(pieces, rounded_w1):
+            name = "%d%d" % pieces[0]
+            codes = tile([P, len(pieces) * WIDE], U32, f"codes{name}")
+            scales = tile([P, len(pieces) * WIDE], U8, f"scales{name}")
+            nc.vector.quantize_mx(out=codes[:].bitcast(FP8X4), scales=scales[:], in_=rounded_w1)
+            for n, piece in enumerate(pieces):
+                quantised[piece] = (codes[:, n * WIDE : (n + 1) * WIDE], scales[:, n * WIDE : (n + 1) * WIDE])
+
+        line = tile([P, 3 * UNIT], BF16, "line")
+
+        def round_pair_scalar(n):
+            place = 2 * (n % 2)
+            round_on_scalar(PAIRS[n][0], line[:, place * UNIT : (place + 1) * UNIT])
+
+        def round_pair_gpsimd(n):
+            round_on_gpsimd(PAIRS[n][1], line[:, UNIT : 2 * UNIT])
+
+        def quantise_pair(n):
+            scalars, gpsimds = PAIRS[n]
+            if scalars is None:
+                quantise_w1([gpsimds], line[:, UNIT : 2 * UNIT])
+            elif n % 2 == 0:
+                quantise_w1([scalars, gpsimds], line[:, : 2 * UNIT])
             else:
-                codes = ring.tile([P, PASS], U32, name="w1_codes", align_bytes=64, bufs=3)
-            if b == H_PASSES - 1 and a > 0:
-                scales = late_scales[ROWS * a :, :]
-            else:
-                scales = ring.tile([P, PASS], U8, name="w1_scales", align_bytes=64, bufs=3)[:]
-            nc.vector.quantize_mx(out=codes[:].bitcast(FP8X4), scales=scales, in_=grouped[:])
-            w1_quantised[a, b] = (codes, scales)
+                quantise_w1([gpsimds, scalars], line[:, UNIT:])
 
         banks = {}
 
-        def first_product(a, b, t):
-            codes, scales = w1_quantised[a, b]
-            for half in range(HALVES):
-                if a == 0:
-                    banks[b, t, half] = psum.tile([P, BANK], F32, name=f"bank{HALVES * t + half}")
-                cols = slice(half * BANK, (half + 1) * BANK)
-                nc.tensor.matmul_mx(
-                    out=banks[b, t, half][:],
-                    lhsT=codes[:, t * P : (t + 1) * P].bitcast(FP8X4),
-                    lhsT_scale=scales[:, t * P : (t + 1) * P],
-                    rhs=v_w[a][:, cols].bitcast(FP8X4),
-                    rhs_scale=v_s[ROWS * a :, cols],
-                    start=(a == 0),
-                    stop=(a == K_PASSES - 1),
-                )
+        def first_product(s, a, half):
+            g, u = divmod(s, PER_GROUP)
+            codes, scales = quantised[g, a]
+            if a == 0:
+                banks[s, half] = psum.tile([P, BANK], F32, name=f"bank{(HALVES * s + half) % 8}")
+            cols = slice(half * BANK, (half + 1) * BANK)
+            nc.tensor.matmul_mx(
+                out=banks[s, half][:],
+                lhsT=codes[:, u * P : (u + 1) * P].bitcast(FP8X4),
+                lhsT_scale=scales[:, u * P : (u + 1) * P],
+                rhs=v_w[a][:, cols].bitcast(FP8X4),
+                rhs_scale=v_s[ROWS * a :, cols],
+                start=(a == 0),
+                stop=(a == K_PASSES - 1),
+            )
 
-        def first_products(b):
-            for t in range(PACK):
-                first_product(0, b, t)
-            for t in range(PACK):
-                for a in range(1, K_PASSES):
-                    first_product(a, b, t)
+        def first_products(g, passes):
+            for s in range(PER_GROUP * g, PER_GROUP * (g + 1)):
+                for a in passes:
+                    for half in range(HALVES):
+                        first_product(s, a, half)
 
         h = {}
         parents = {}
 
-        def fetch_parents(b, t):
-            h[b, t] = keep.tile([P, S], F32, name=f"h{b}{t}")
+        def copy_h(s):
+            h[s] = tile([P, S], F32, f"h{s}")
             for half in range(HALVES):
-                nc.scalar.copy(h[b, t][:, half * BANK : (half + 1) * BANK], banks[b, t, half][:])
-            parents[b, t] = keep.tile([P, M], F32, name=f"parents{b}{t}", tag=f"parents{b}{t}", align_bytes=64)
-            nc.vector.tensor_copy(parents[b, t][:], h[b, t][:].indirect(pos1_sb[:]))
+                dst = h[s][:, half * BANK : (half + 1) * BANK]
+                if (s, half) == (0, 1):
+                    nc.vector.tensor_copy(dst, banks[s, half][:])
+                else:
+                    nc.scalar.copy(dst, banks[s, half][:])
+
+        def fetch_parents(s):
+            parents[s] = tile([P, M], F32, f"parents{s}")
+            nc.vector.tensor_copy(parents[s][:], h[s][:].indirect(pos1_sb[:]))
+
+        dealt = [tile([P, PACK, M], BF16, f"dealt{b}", f"raw0{b}") for b in range(H_PASSES)]
+        rounded = tile([P, SLICES, M], BF16, "rounded")
+        squashed = {}
+
+        def squash(slices, tag):
+            room = tile([P, len(slices), M], F32, f"squashed{slices[0]}", tag)
+            for n, s in enumerate(slices):
+                squashed[s] = room[:, n, :]
+                nc.scalar.activation(squashed[s], parents[s][:], ACT.Tanh)
+                gain = factors[:, s : s + 1]
+                if s == SLICES - 1:
+                    nc.scalar.activation(rounded[:, s, :], squashed[s], ACT.Copy, scale=gain)
+                else:
+                    nc.gpsimd.tensor_scalar(rounded[:, s, :], squashed[s], gain, 0.0, ALU.mult, ALU.add)
+                b, quad = divmod(s, QUADS)
+                nc.sync.dma_start(
+                    out=dealt[b][32 * quad : 32 * (quad + 1)].rearrange("q t m -> q (t m)").bitcast(I32),
+                    in_=rounded[:, s, :].bitcast(I32),
+                )
 
         x_grouped = {}
         x_codes = {}
-        x_scales = [keep.tile([P, M], U8, name=f"x_scales{b}", align_bytes=64) for b in range(H_PASSES)]
+        x_scales = [tile([P, M], U8, f"x_scales{b}") for b in range(H_PASSES)]
 
-        def make_x(b):
-            rounded = ring.tile([P, PACK, M], BF16, name="x_rounded", bufs=H_PASSES)
-            if b == 0:
-                squashed = w1_raw[K_PASSES - 1, H_PASSES - 1]
+        def interleave_x(b):
+            x_grouped[b] = tile([P, M * PACK], BF16, f"x_grouped{b}", f"raw1{b}")
+            dst = x_grouped[b][:].rearrange("p (c i t) -> p c t i", i=4, t=PACK)
+            src = dealt[b][:].rearrange("p t (c i) -> p c t i", i=4)
+            if b == H_PASSES - 1:
+                cut = SCALAR_CUT // 4
+                nc.scalar.copy(dst[:, :cut], src[:, :cut])
+                nc.vector.tensor_copy(dst[:, cut:], src[:, cut:])
             else:
-                squashed = keep.tile([P, PACK, M], F32, name="squashed", tag="last_codes", align_bytes=64)
-            for t in range(PACK):
-                nc.scalar.activation(squashed[:, t, :], parents[b, t][:], ACT.Tanh)
-                gain = gn_sb[:, b, t : t + 1]
-                if (b, t) == LAST_SLICE:
-                    nc.scalar.activation(rounded[:, t, :], squashed[:, t, :], ACT.Copy, scale=gain)
-                else:
-                    nc.gpsimd.tensor_scalar(rounded[:, t, :], squashed[:, t, :], gain, 0.0, ALU.mult, ALU.add)
-            grouped = x_grouped[b] = ring.tile([P, M * PACK], BF16, name="x_grouped", align_bytes=64, bufs=H_PASSES)
-            cut = M // 2 if b == H_PASSES - 1 else 0
-            if cut:
-                nc.scalar.copy(
-                    grouped[:, : PACK * cut].rearrange("p (c i t) -> p c t i", i=4, t=PACK),
-                    rounded[:, :, :cut].rearrange("p t (c i) -> p c t i", i=4),
-                )
-                nc.vector.tensor_copy(
-                    grouped[:, PACK * cut :].rearrange("p (c i t) -> p c t i", i=4, t=PACK),
-                    rounded[:, :, cut:].rearrange("p t (c i) -> p c t i", i=4),
-                )
-            else:
-                nc.gpsimd.tensor_scalar(
-                    grouped[:].rearrange("p (m t) -> p m t", t=PACK),
-                    rounded[:].rearrange("p t m -> p m t"),
-                    1.0,
-                    0.0,
-                    ALU.mult,
-                    ALU.add,
-                )
+                cut = X0_SCALAR_CUT
+                nc.scalar.copy(dst[:, : cut // 4], src[:, : cut // 4])
+                dst = x_grouped[b][:].rearrange("p (m t) -> p m t", t=PACK)[:, cut:]
+                src = dealt[b][:].rearrange("p t m -> p m t")[:, cut:]
+                nc.gpsimd.tensor_scalar(dst, src, 1.0, 0.0, ALU.mult, ALU.add)
 
         def quantise_x(b):
-            tag = "parents10" if b == 0 else "x_codes1"
-            x_codes[b] = keep.tile([P, M], U32, name=f"x_codes{b}", tag=tag, align_bytes=64)
+            x_codes[b] = tile([P, M], U32, f"x_codes{b}")
             nc.vector.quantize_mx(out=x_codes[b][:].bitcast(FP8X4), scales=x_scales[b][:], in_=x_grouped[b][:])
+
+        skip = {}
+
+        def fetch_skip(s, room):
+            skip[s] = room
+            nc.vector.tensor_copy(room, h[s][:].indirect(pos2_sb[:]))
 
         gather_table(0)
         nc.vector.tensor_copy(v_s[:], tab_s[:].indirect(offs_sb[:]))
-        quantise_w1(0, 0)
-        w2p_s = keep.tile([P, H_PASSES * H], U8, name="w2p_s", align_bytes=64)
-        nc.vector.tensor_copy(
-            w2p_s[:].rearrange("p (g t u v) -> p g u t v", t=PACK, u=8, v=16),
-            w2_s[:].rearrange("p (g u v t) -> p g u t v", t=PACK, u=8, v=16),
-        )
+        for a in range(K_PASSES):
+            unit = tile([P, UNIT], BF16, f"unit{a}")
+            round_on_scalar((0, a), unit[:])
+            quantise_w1([(0, a)], unit[:])
         for a in range(1, K_PASSES):
             gather_table(a)
-            quantise_w1(a, 0)
-        w2p_w = keep.tile([P, H_PASSES * H * 2], U8, name="w2p_w", align_bytes=64)
-        nc.vector.tensor_copy(
-            w2p_w[:].bitcast(U16).rearrange("p (g t u v) -> p g u t v", t=PACK, u=16, v=8),
-            w2_w[:].bitcast(U16).rearrange("p (g u v t) -> p g u t v", t=PACK, u=16, v=8),
-        )
-        first_products(0)
-        fetch_parents(0, 0)
-        quantise_w1(0, 1)
-        for t in range(1, PACK):
-            fetch_parents(0, t)
-        for a in range(1, K_PASSES):
-            quantise_w1(a, 1)
-        first_products(1)
-        for t in range(PACK):
-            fetch_parents(1, t)
-        for b in range(H_PASSES):
-            make_x(b)
-        for b in range(H_PASSES):
-            quantise_x(b)
+        for a in range(K_PASSES):
+            for half in range(HALVES):
+                for s in range(PER_GROUP):
+                    first_product(s, a, half)
+        round_pair_scalar(0)
+        round_pair_gpsimd(0)
+        copy_h(0)
+        copy_h(1)
+        quantise_pair(0)
+        first_products(1, [0, 1])
+        fetch_parents(0)
+        round_pair_scalar(1)
+        round_pair_gpsimd(1)
+        quantise_pair(1)
+        first_products(1, [2])
+        first_products(2, [0])
+        fetch_parents(1)
+        round_pair_scalar(2)
+        round_pair_gpsimd(2)
+        copy_h(2)
+        copy_h(3)
+        quantise_pair(2)
+        first_products(2, [1, 2])
+        fetch_parents(2)
+        fetch_parents(3)
+        round_pair_scalar(3)
+        round_pair_gpsimd(3)
+        quantise_pair(3)
+        first_products(3, [0, 1])
+        copy_h(4)
+        copy_h(5)
+        fetch_parents(4)
+        round_pair_gpsimd(4)
+        quantise_pair(4)
+        first_products(3, [2])
+        fetch_parents(5)
+        copy_h(6)
+        copy_h(7)
+        fetch_parents(6)
+        fetch_parents(7)
+        squash([0, 1], "raw32")
+        squash([2, 3, 4, 5, 6, 7], "codes32")
+        interleave_x(0)
+        quantise_x(0)
+        interleave_x(1)
+        quantise_x(1)
 
-        skip_room = [
-            w1_grouped[1, 1][:].bitcast(F32)[:, :M],
-            w1_grouped[2, 1][:].bitcast(F32)[:, :M],
-            w1_grouped[2, 1][:].bitcast(F32)[:, M:],
-            parents[1, 1][:],
-            x_grouped[1][:].bitcast(F32)[:, :M],
-        ]
-        skip_room = skip_room + skip_room[1:4]
-
-        rooms = [keep.tile([P, H // P, M], F32, name=f"room{a}", tag=f"tab_w{a}") for a in range(K_PASSES)]
-        out_rows = out.rearrange("(b p t) m -> b t p m", p=P, t=PACK)
-        for b in range(H_PASSES):
-            for t in range(PACK):
-                number = PACK * b + t
-                skip = skip_room[number]
-                nc.vector.tensor_copy(skip, h[b, t][:].indirect(pos2_sb[:]))
-                y = psum.tile([P, BANK], F32, name=f"bank{number}")
-                for a in range(H_PASSES):
-                    col = a * H + b * PASS + t * P
-                    nc.tensor.matmul_mx(
-                        out=y[:],
-                        lhsT=w2p_w[:, 2 * col : 2 * (col + P)].bitcast(FP4X4),
-                        lhsT_scale=w2p_s[:, col : col + P],
-                        rhs=x_codes[a][:].bitcast(FP8X4),
-                        rhs_scale=x_scales[a][:],
-                        start=(a == 0),
-                        stop=(a == H_PASSES - 1),
-                    )
-                z, gated, res = (room[:, number, :] for room in rooms)
-                adder = nc.gpsimd if number < GPSIMD_SUMS else nc.vector
-                width = M // 2 if (b, t) == LAST_SLICE else M
-                parts = [slice(c, c + width) for c in range(0, M, width)]
-                for cols in parts:
-                    nc.vector.scalar_tensor_tensor(
-                        z[:, cols], skip[:, cols], rs_sb[:, b, t : t + 1], y[:, cols], ALU.mult, ALU.add
-                    )
-                    nc.scalar.activation(gated[:, cols], z[:, cols], ACT.Silu)
-                for cols in parts:
-                    adder.tensor_tensor(res[:, cols], gated[:, cols], z[:, cols], ALU.add)
-                    nc.sync.dma_start(out=out_rows[b, t][:, cols], in_=res[:, cols])
+        first_room = tile([P, M], F32, "first_room", "raw21")
+        skip_room = [first_room[:]] + [parents[s][:] for s in range(2, 6)] + [x_grouped[1][:].bitcast(F32)[:, :M]]
+        skip_room = skip_room + skip_room[:2]
+        rooms = [tile([P, SLICES, M], F32, f"room{a}", f"tab_w{a}") for a in range(K_PASSES)]
+        for s in range(6):
+            fetch_skip(s, skip_room[s])
+        for s in range(SLICES):
+            if 1 <= s <= 2:
+                fetch_skip(5 + s, skip_room[5 + s])
+            y = psum.tile([P, BANK], F32, name=f"bank{s}")
+            for a in range(H_PASSES):
+                col = a * H + s * P
+                nc.tensor.matmul_mx(
+                    out=y[:],
+                    lhsT=w2_w[:, 2 * col : 2 * (col + P)].bitcast(FP4X4),
+                    lhsT_scale=w2_s[:, col : col + P],
+                    rhs=x_codes[a][:].bitcast(FP8X4),
+                    rhs_scale=x_scales[a][:],
+                    start=(a == 0),
+                    stop=(a == H_PASSES - 1),
+                )
+            z, gated, res = (room[:, s, :] for room in rooms)
+            adder = nc.gpsimd if s < GPSIMD_SUMS else nc.vector
+            width = M // 2 if s == SLICES - 1 else M
+            parts = [slice(c, c + width) for c in range(0, M, width)]
+            weight = factors[:, SLICES + s : SLICES + s + 1]
+            for cols in parts:
+                nc.vector.scalar_tensor_tensor(z[:, cols], skip[s][:, cols], weight, y[:, cols], ALU.mult, ALU.add)
+                nc.scalar.activation(gated[:, cols], z[:, cols], ACT.Silu)
+            for cols in parts:
+                adder.tensor_tensor(res[:, cols], gated[:, cols], z[:, cols], ALU.add)
+                nc.sync.dma_start(out=out[s * P : (s + 1) * P, cols], in_=res[:, cols])

@@ -31,9 +31,9 @@ SLICES = H // P
 WIDE = 256
 GROUPS = H // WIDE
 PER_GROUP = WIDE // P
-PAIRS = [((1, 0), (1, 1)), ((1, 2), (2, 0)), ((2, 1), (2, 2)), ((3, 0), (3, 1)), (None, (3, 2))]
 UNIT = PACK * WIDE
 GPSIMD_SUMS = 6
+Y_BANKS = 4
 SCALAR_CUT = 176
 X0_SCALAR_CUT = 320
 
@@ -121,9 +121,12 @@ def tile_list_fiddle_phrase_variation_kernel(
 
         quantised = {}
 
-        def round_on_scalar(piece, unit):
+        def round_on(copy, piece, unit):
             src = raw[piece][:].rearrange("p j (c i) -> p c j i", i=4)
-            nc.scalar.copy(unit.rearrange("p (c i j) -> p c j i", i=4, j=PACK), src)
+            copy(unit.rearrange("p (c i j) -> p c j i", i=4, j=PACK), src)
+
+        def round_on_scalar(piece, unit):
+            round_on(nc.scalar.copy, piece, unit)
 
         def round_on_gpsimd(piece, unit):
             src = raw[piece][:].rearrange("p j c -> p c j")
@@ -137,23 +140,10 @@ def tile_list_fiddle_phrase_variation_kernel(
             for n, piece in enumerate(pieces):
                 quantised[piece] = (codes[:, n * WIDE : (n + 1) * WIDE], scales[:, n * WIDE : (n + 1) * WIDE])
 
-        line = tile([P, 3 * UNIT], BF16, "line")
+        line = tile([P, 4 * UNIT], BF16, "line")
 
-        def round_pair_scalar(n):
-            place = 2 * (n % 2)
-            round_on_scalar(PAIRS[n][0], line[:, place * UNIT : (place + 1) * UNIT])
-
-        def round_pair_gpsimd(n):
-            round_on_gpsimd(PAIRS[n][1], line[:, UNIT : 2 * UNIT])
-
-        def quantise_pair(n):
-            scalars, gpsimds = PAIRS[n]
-            if scalars is None:
-                quantise_w1([gpsimds], line[:, UNIT : 2 * UNIT])
-            elif n % 2 == 0:
-                quantise_w1([scalars, gpsimds], line[:, : 2 * UNIT])
-            else:
-                quantise_w1([gpsimds, scalars], line[:, UNIT:])
+        def units(first, count=1):
+            return line[:, first * UNIT : (first + count) * UNIT]
 
         banks = {}
 
@@ -186,41 +176,37 @@ def tile_list_fiddle_phrase_variation_kernel(
             h[s] = tile([P, S], F32, f"h{s}")
             for half in range(HALVES):
                 dst = h[s][:, half * BANK : (half + 1) * BANK]
-                if (s, half) == (0, 1):
-                    nc.vector.tensor_copy(dst, banks[s, half][:])
-                else:
-                    nc.scalar.copy(dst, banks[s, half][:])
+                nc.scalar.copy(dst, banks[s, half][:])
 
-        def fetch_parents(s):
-            parents[s] = tile([P, M], F32, f"parents{s}")
-            nc.vector.tensor_copy(parents[s][:], h[s][:].indirect(pos1_sb[:]))
+        def fetch_parents(s, room=None):
+            parents[s] = tile([P, M], F32, f"parents{s}")[:] if room is None else room
+            nc.vector.tensor_copy(parents[s], h[s][:].indirect(pos1_sb[:]))
 
         dealt = [tile([P, PACK, M], BF16, f"dealt{b}", f"raw0{b}") for b in range(H_PASSES)]
-        rounded = tile([P, SLICES, M], BF16, "rounded")
         squashed = {}
 
-        def squash(slices, tag):
-            room = tile([P, len(slices), M], F32, f"squashed{slices[0]}", tag)
-            for n, s in enumerate(slices):
-                squashed[s] = room[:, n, :]
-                nc.scalar.activation(squashed[s], parents[s][:], ACT.Tanh)
-                gain = factors[:, s : s + 1]
-                if s == SLICES - 1:
-                    nc.scalar.activation(rounded[:, s, :], squashed[s], ACT.Copy, scale=gain)
-                else:
-                    nc.gpsimd.tensor_scalar(rounded[:, s, :], squashed[s], gain, 0.0, ALU.mult, ALU.add)
-                b, quad = divmod(s, QUADS)
-                nc.sync.dma_start(
-                    out=dealt[b][32 * quad : 32 * (quad + 1)].rearrange("q t m -> q (t m)").bitcast(I32),
-                    in_=rounded[:, s, :].bitcast(I32),
-                )
+        def squash(s, room):
+            squashed[s] = room
+            nc.scalar.activation(room, parents[s], ACT.Tanh)
+
+        def gain_and_deal(s, rounded):
+            gain = factors[:, s : s + 1]
+            if s == SLICES - 1:
+                nc.scalar.activation(rounded, squashed[s], ACT.Copy, scale=gain)
+            else:
+                nc.gpsimd.tensor_scalar(rounded, squashed[s], gain, 0.0, ALU.mult, ALU.add)
+            b, quad = divmod(s, QUADS)
+            nc.sync.dma_start(
+                out=dealt[b][32 * quad : 32 * (quad + 1)].rearrange("q t m -> q (t m)").bitcast(I32),
+                in_=rounded.bitcast(I32),
+            )
 
         x_grouped = {}
         x_codes = {}
         x_scales = [tile([P, M], U8, f"x_scales{b}") for b in range(H_PASSES)]
 
         def interleave_x(b):
-            x_grouped[b] = tile([P, M * PACK], BF16, f"x_grouped{b}", f"raw1{b}")
+            x_grouped[b] = tile([P, M * PACK], BF16, f"x_grouped{b}", f"raw2{2 * b}")
             dst = x_grouped[b][:].rearrange("p (c i t) -> p c t i", i=4, t=PACK)
             src = dealt[b][:].rearrange("p t (c i) -> p c t i", i=4)
             if b == H_PASSES - 1:
@@ -256,59 +242,66 @@ def tile_list_fiddle_phrase_variation_kernel(
             for half in range(HALVES):
                 for s in range(PER_GROUP):
                     first_product(s, a, half)
-        round_pair_scalar(0)
-        round_pair_gpsimd(0)
+        pair = tile([P, 2 * UNIT], BF16, "pair")
+        round_on_gpsimd((1, 0), pair[:, :UNIT])
+        round_on(nc.vector.tensor_copy, (1, 1), pair[:, UNIT:])
         copy_h(0)
         copy_h(1)
-        quantise_pair(0)
+        quantise_w1([(1, 0), (1, 1)], pair[:])
         first_products(1, [0, 1])
-        fetch_parents(0)
-        round_pair_scalar(1)
-        round_pair_gpsimd(1)
-        quantise_pair(1)
+        fetch_parents(0, pair[:, :UNIT].bitcast(F32))
+        round_on_scalar((1, 2), units(0))
+        round_on_gpsimd((2, 0), units(1))
+        quantise_w1([(1, 2), (2, 0)], units(0, 2))
         first_products(1, [2])
         first_products(2, [0])
-        fetch_parents(1)
-        round_pair_scalar(2)
-        round_pair_gpsimd(2)
+        fetch_parents(1, units(0).bitcast(F32))
+        round_on_scalar((2, 1), units(2))
+        round_on_gpsimd((2, 2), units(1))
         copy_h(2)
         copy_h(3)
-        quantise_pair(2)
+        quantise_w1([(2, 2), (2, 1)], units(1, 2))
         first_products(2, [1, 2])
-        fetch_parents(2)
+        fetch_parents(2, units(1).bitcast(F32))
         fetch_parents(3)
-        round_pair_scalar(3)
-        round_pair_gpsimd(3)
-        quantise_pair(3)
-        first_products(3, [0, 1])
+        round_on_gpsimd((3, 0), units(2))
+        round_on_gpsimd((3, 1), units(3))
         copy_h(4)
         copy_h(5)
-        fetch_parents(4)
-        round_pair_gpsimd(4)
-        quantise_pair(4)
+        quantise_w1([(3, 0), (3, 1)], units(2, 2))
+        first_products(3, [0, 1])
+        fetch_parents(4, units(3).bitcast(F32))
+        round_on_gpsimd((3, 2), units(2))
+        quantise_w1([(3, 2)], units(2))
         first_products(3, [2])
-        fetch_parents(5)
-        copy_h(6)
-        copy_h(7)
-        fetch_parents(6)
-        fetch_parents(7)
-        squash([0, 1], "raw32")
-        squash([2, 3, 4, 5, 6, 7], "codes32")
+        last_room = tile([P, 2, M], F32, "last_room", "raw32")
+        fetch_parents(5, last_room[:, 0, :])
+        for s in range(6, SLICES):
+            copy_h(s)
+            fetch_parents(s)
+        squash(0, tile([P, M], F32, "squashed0", "raw21")[:])
+        middle = tile([P, 4, M], F32, "middle", "raw31")
+        late = tile([P, 3, M], F32, "late", "scales32")
+        rounded = tile([P, SLICES - 2, M], BF16, "rounded", "codes32")
+        for s in range(1, SLICES):
+            squash(s, middle[:, s - 1, :] if s <= 4 else late[:, s - 5, :])
+        for s in range(SLICES):
+            gain_and_deal(s, units(2)[:, s * M : (s + 1) * M] if s < 2 else rounded[:, s - 2, :])
         interleave_x(0)
         quantise_x(0)
         interleave_x(1)
         quantise_x(1)
 
-        first_room = tile([P, M], F32, "first_room", "raw21")
-        skip_room = [first_room[:]] + [parents[s][:] for s in range(2, 6)] + [x_grouped[1][:].bitcast(F32)[:, :M]]
-        skip_room = skip_room + skip_room[:2]
+        skip_room = [last_room[:, 1, :], parents[5], parents[6], parents[7], x_grouped[1][:].bitcast(F32)[:, :M]]
+        skip_room = skip_room + skip_room[3:5] + skip_room[3:4]
         rooms = [tile([P, SLICES, M], F32, f"room{a}", f"tab_w{a}") for a in range(K_PASSES)]
-        for s in range(6):
+        sums = []
+        for s in range(5):
             fetch_skip(s, skip_room[s])
         for s in range(SLICES):
-            if 1 <= s <= 2:
-                fetch_skip(5 + s, skip_room[5 + s])
-            y = psum.tile([P, BANK], F32, name=f"bank{s}")
+            if s >= 5:
+                fetch_skip(s, skip_room[s])
+            y = psum.tile([P, BANK], F32, name=f"bank{s % Y_BANKS}")
             for a in range(H_PASSES):
                 col = a * H + s * P
                 nc.tensor.matmul_mx(
@@ -329,5 +322,7 @@ def tile_list_fiddle_phrase_variation_kernel(
                 nc.vector.scalar_tensor_tensor(z[:, cols], skip[s][:, cols], weight, y[:, cols], ALU.mult, ALU.add)
                 nc.scalar.activation(gated[:, cols], z[:, cols], ACT.Silu)
             for cols in parts:
-                adder.tensor_tensor(res[:, cols], gated[:, cols], z[:, cols], ALU.add)
-                nc.sync.dma_start(out=out[s * P : (s + 1) * P, cols], in_=res[:, cols])
+                sums.append((adder, res[:, cols], gated[:, cols], z[:, cols], out[s * P : (s + 1) * P, cols]))
+        for adder, res, gated, z, rows in sums:
+            adder.tensor_tensor(res, gated, z, ALU.add)
+            nc.sync.dma_start(out=rows, in_=res)

@@ -64,8 +64,9 @@ def tile_list_fiddle_phrase_variation_kernel(
         nc.vector.memset(staged[:], 0.0)
         nc.vector.memset(w2_s[:].bitcast(I32), 0)
 
-        def load_table(a):
-            nc.sync.dma_start(out=tab_w[a][:], in_=tab_words[a].rearrange("p t i -> p (t i)").bitcast(I32))
+        def load_table(a, cols=slice(0, T)):
+            words = tab_words[a].rearrange("p t i -> p (t i)").bitcast(I32)
+            nc.sync.dma_start(out=tab_w[a][:, cols], in_=words[:, cols])
 
         raw = {}
 
@@ -86,9 +87,10 @@ def tile_list_fiddle_phrase_variation_kernel(
         nc.sync.dma_start(pos2_sb[:], pos2)
         load_w1(0, 1)
         load_w1(0, 2)
+        load_table(1, slice(0, T // 2))
         nc.sync.dma_start(out=staged[:SLICES, :], in_=gn.rearrange("(s p) -> s p", p=P))
         nc.sync.dma_start(out=staged[SLICES : 2 * SLICES, :], in_=rs.rearrange("(s p) -> s p", p=P))
-        load_table(1)
+        load_table(1, slice(T // 2, T))
         load_table(2)
         for g in range(1, GROUPS):
             for a in range(K_PASSES):

@@ -32,7 +32,7 @@ WIDE = 256
 GROUPS = H // WIDE
 PER_GROUP = WIDE // P
 UNIT = PACK * WIDE
-GPSIMD_SUMS = 6
+GPSIMD_SUMS = 5
 Y_BANKS = 4
 SCALAR_CUT = 176
 X0_SCALAR_CUT = 320
@@ -47,7 +47,7 @@ def tile_list_fiddle_phrase_variation_kernel(
         psum = ctx.enter_context(tc.psum_pool(name="psum", bufs=1))
 
         def tile(shape, dtype, name, tag=None):
-            return keep.tile(shape, dtype, name=name, tag=tag or name, align_bytes=64)
+            return keep.tile(shape, dtype, name=name, tag=tag or name, align_bytes=256)
 
         offs_sb = keep.tile([P, S // PER_COLUMN], U16, name="offs_sb")
         pos1_sb = keep.tile([P, M // PER_COLUMN], U16, name="pos1_sb")
@@ -142,10 +142,10 @@ def tile_list_fiddle_phrase_variation_kernel(
             for n, piece in enumerate(pieces):
                 quantised[piece] = (codes[:, n * WIDE : (n + 1) * WIDE], scales[:, n * WIDE : (n + 1) * WIDE])
 
-        line = tile([P, 4 * UNIT], BF16, "line")
+        line = tile([P, 13 * M], BF16, "line")
 
-        def units(first, count=1):
-            return line[:, first * UNIT : (first + count) * UNIT]
+        def place(first, count=2):
+            return line[:, first * M : (first + count) * M]
 
         banks = {}
 
@@ -232,6 +232,14 @@ def tile_list_fiddle_phrase_variation_kernel(
             skip[s] = room
             nc.vector.tensor_copy(room, h[s][:].indirect(pos2_sb[:]))
 
+        def fetch_half_skip(s, room, half):
+            skip[s] = room
+            columns = M // PER_COLUMN // 2
+            nc.vector.tensor_copy(
+                room[:, half * M // 2 : (half + 1) * M // 2],
+                h[s][:].indirect(pos2_sb[:, half * columns : (half + 1) * columns]),
+            )
+
         gather_table(0)
         nc.vector.tensor_copy(v_s[:], tab_s[:].indirect(offs_sb[:]))
         for a in range(K_PASSES):
@@ -244,37 +252,38 @@ def tile_list_fiddle_phrase_variation_kernel(
             for half in range(HALVES):
                 for s in range(PER_GROUP):
                     first_product(s, a, half)
-        pair = tile([P, 2 * UNIT], BF16, "pair")
-        round_on_gpsimd((1, 0), pair[:, :UNIT])
-        round_on(nc.vector.tensor_copy, (1, 1), pair[:, UNIT:])
+        round_on_gpsimd((1, 0), place(0))
+        round_on(nc.vector.tensor_copy, (1, 1), place(2))
         copy_h(0)
         copy_h(1)
-        quantise_w1([(1, 0), (1, 1)], pair[:])
+        quantise_w1([(1, 0), (1, 1)], place(0, 4))
         first_products(1, [0, 1])
-        fetch_parents(0, pair[:, :UNIT].bitcast(F32))
-        round_on_scalar((1, 2), units(0))
-        round_on_gpsimd((2, 0), units(1))
-        quantise_w1([(1, 2), (2, 0)], units(0, 2))
+        fetch_parents(0, place(0).bitcast(F32))
+        fetch_half_skip(0, place(3).bitcast(F32), 0)
+        round_on_scalar((1, 2), place(4))
+        round_on_gpsimd((2, 0), place(6))
+        quantise_w1([(1, 2), (2, 0)], place(4, 4))
         first_products(1, [2])
         first_products(2, [0])
-        fetch_parents(1, units(0).bitcast(F32))
-        round_on_scalar((2, 1), units(2))
-        round_on_gpsimd((2, 2), units(1))
+        fetch_parents(1, place(5).bitcast(F32))
+        fetch_half_skip(0, place(3).bitcast(F32), 1)
+        round_on_scalar((2, 1), place(9))
+        round_on_gpsimd((2, 2), place(7))
         copy_h(2)
         copy_h(3)
-        quantise_w1([(2, 2), (2, 1)], units(1, 2))
+        quantise_w1([(2, 2), (2, 1)], place(7, 4))
         first_products(2, [1, 2])
-        fetch_parents(2, units(1).bitcast(F32))
+        fetch_parents(2, place(7).bitcast(F32))
         fetch_parents(3)
-        round_on_gpsimd((3, 0), units(2))
-        round_on_gpsimd((3, 1), units(3))
+        round_on_gpsimd((3, 0), place(9))
+        round_on_gpsimd((3, 1), place(11))
         copy_h(4)
         copy_h(5)
-        quantise_w1([(3, 0), (3, 1)], units(2, 2))
+        quantise_w1([(3, 0), (3, 1)], place(9, 4))
         first_products(3, [0, 1])
-        fetch_parents(4, units(3).bitcast(F32))
-        round_on_gpsimd((3, 2), units(2))
-        quantise_w1([(3, 2)], units(2))
+        fetch_parents(4, place(11).bitcast(F32))
+        round_on_gpsimd((3, 2), place(9))
+        quantise_w1([(3, 2)], place(9))
         first_products(3, [2])
         last_room = tile([P, 2, M], F32, "last_room", "raw32")
         fetch_parents(5, last_room[:, 0, :])
@@ -288,20 +297,21 @@ def tile_list_fiddle_phrase_variation_kernel(
         for s in range(1, SLICES):
             squash(s, middle[:, s - 1, :] if s <= 4 else late[:, s - 5, :])
         for s in range(SLICES):
-            gain_and_deal(s, units(2)[:, s * M : (s + 1) * M] if s < 2 else rounded[:, s - 2, :])
+            gain_and_deal(s, place(9 + s, 1) if s < 2 else rounded[:, s - 2, :])
         interleave_x(0)
         quantise_x(0)
         interleave_x(1)
         quantise_x(1)
 
-        skip_room = [last_room[:, 1, :], parents[5], parents[6], parents[7], x_grouped[1][:].bitcast(F32)[:, :M]]
-        skip_room = skip_room + skip_room[3:5] + skip_room[3:4]
+        skip_room = [skip[0], last_room[:, 1, :], parents[5], parents[6], parents[7]]
+        skip_room = skip_room + [x_grouped[1][:].bitcast(F32)[:, :M]]
+        skip_room = skip_room + skip_room[4:6]
         rooms = [tile([P, SLICES, M], F32, f"room{a}", f"tab_w{a}") for a in range(K_PASSES)]
         sums = []
-        for s in range(5):
+        for s in range(1, 6):
             fetch_skip(s, skip_room[s])
         for s in range(SLICES):
-            if s >= 5:
+            if s >= 6:
                 fetch_skip(s, skip_room[s])
             y = psum.tile([P, BANK], F32, name=f"bank{s % Y_BANKS}")
             for a in range(H_PASSES):

@@ -33,6 +33,8 @@ GROUPS = H // WIDE
 PER_GROUP = WIDE // P
 UNIT = PACK * WIDE
 GPSIMD_SUMS = 5
+TENSOR_SUM = 1
+TENSOR_LAG = 4
 Y_BANKS = 4
 SCALAR_CUT = 176
 X0_SCALAR_CUT = 320
@@ -308,6 +310,22 @@ def tile_list_fiddle_phrase_variation_kernel(
         skip_room = skip_room + skip_room[4:6]
         rooms = [tile([P, SLICES, M], F32, f"room{a}", f"tab_w{a}") for a in range(K_PASSES)]
         sums = []
+
+        middle_sum = tile([P, M], F32, "middle_sum", "h0")
+
+        def add_on_tensor(res, gated, z, rows):
+            there = psum.tile([P, BANK], F32, name=f"bank{Y_BANKS}")
+            back = psum.tile([P, BANK], F32, name=f"bank{Y_BANKS + 1}")
+            for c in range(0, M, P):
+                cols = slice(c, c + P)
+                nc.tensor.matmul(there[:, cols], z[:, cols], identity[:], start=True, stop=False, is_transpose=True)
+                nc.tensor.matmul(there[:, cols], gated[:, cols], identity[:], start=False, stop=True, is_transpose=True)
+            nc.scalar.copy(middle_sum[:], there[:])
+            for c in range(0, M, P):
+                nc.tensor.transpose(back[:, c : c + P], middle_sum[:, c : c + P], identity[:])
+            nc.scalar.copy(res, back[:])
+            nc.sync.dma_start(out=rows, in_=res)
+
         for s in range(1, 6):
             fetch_skip(s, skip_room[s])
         for s in range(SLICES):
@@ -326,6 +344,8 @@ def tile_list_fiddle_phrase_variation_kernel(
                     stop=(a == H_PASSES - 1),
                 )
             z, gated, res = (room[:, s, :] for room in rooms)
+            if s == TENSOR_SUM + TENSOR_LAG + 1:
+                gated = middle_sum[:]
             adder = nc.gpsimd if s < GPSIMD_SUMS else nc.vector
             width = M // 2 if s == SLICES - 1 else M
             parts = [slice(c, c + width) for c in range(0, M, width)]
@@ -333,6 +353,11 @@ def tile_list_fiddle_phrase_variation_kernel(
             for cols in parts:
                 nc.vector.scalar_tensor_tensor(z[:, cols], skip[s][:, cols], weight, y[:, cols], ALU.mult, ALU.add)
                 nc.scalar.activation(gated[:, cols], z[:, cols], ACT.Silu)
+            if s == TENSOR_SUM:
+                turned_sum = (res, gated, z)
+                continue
+            if s == TENSOR_SUM + TENSOR_LAG:
+                add_on_tensor(*turned_sum, out[TENSOR_SUM * P : (TENSOR_SUM + 1) * P, :])
             for cols in parts:
                 sums.append((adder, res[:, cols], gated[:, cols], z[:, cols], out[s * P : (s + 1) * P, cols]))
         for adder, res, gated, z, rows in sums:

@@ -210,7 +210,7 @@ def tile_list_fiddle_phrase_variation_kernel(
         x_scales = [tile([P, M], U8, f"x_scales{b}") for b in range(H_PASSES)]
 
         def interleave_x(b):
-            x_grouped[b] = tile([P, M * PACK], BF16, f"x_grouped{b}", f"raw2{2 * b}")
+            x_grouped[b] = tile([P, M * PACK], BF16, "x_grouped0", "raw20") if b == 0 else place(5, PACK)
             dst = x_grouped[b][:].rearrange("p (c i t) -> p c t i", i=4, t=PACK)
             src = dealt[b][:].rearrange("p t (c i) -> p c t i", i=4)
             if b == H_PASSES - 1:
@@ -261,14 +261,14 @@ def tile_list_fiddle_phrase_variation_kernel(
         quantise_w1([(1, 0), (1, 1)], place(0, 4))
         first_products(1, [0, 1])
         fetch_parents(0, place(0).bitcast(F32))
-        fetch_half_skip(0, place(3).bitcast(F32), 0)
+        fetch_skip(0, tile([P, M], F32, "skip0", "raw11")[:])
         round_on_scalar((1, 2), place(4))
         round_on_gpsimd((2, 0), place(6))
         quantise_w1([(1, 2), (2, 0)], place(4, 4))
         first_products(1, [2])
         first_products(2, [0])
         fetch_parents(1, place(5).bitcast(F32))
-        fetch_half_skip(0, place(3).bitcast(F32), 1)
+        fetch_half_skip(1, place(4).bitcast(F32), 0)
         round_on_scalar((2, 1), place(9))
         round_on_gpsimd((2, 2), place(7))
         copy_h(2)
@@ -305,8 +305,7 @@ def tile_list_fiddle_phrase_variation_kernel(
         interleave_x(1)
         quantise_x(1)
 
-        skip_room = [skip[0], last_room[:, 1, :], parents[5], parents[6], parents[7]]
-        skip_room = skip_room + [x_grouped[1][:].bitcast(F32)[:, :M]]
+        skip_room = [skip[0], skip[1], last_room[:, 1, :], parents[5], parents[6], parents[7]]
         skip_room = skip_room + skip_room[4:6]
         rooms = [tile([P, SLICES, M], F32, f"room{a}", f"tab_w{a}") for a in range(K_PASSES)]
         sums = []
@@ -326,8 +325,9 @@ def tile_list_fiddle_phrase_variation_kernel(
             nc.scalar.copy(res, back[:])
             nc.sync.dma_start(out=rows, in_=res)
 
-        for s in range(1, 6):
+        for s in range(2, 6):
             fetch_skip(s, skip_room[s])
+        fetch_half_skip(1, skip[1], 1)
         for s in range(SLICES):
             if s >= 6:
                 fetch_skip(s, skip_room[s])

@@ -133,8 +133,9 @@ def tile_list_fiddle_phrase_variation_kernel(
             round_on(nc.scalar.copy, piece, unit)
 
         def round_on_gpsimd(piece, unit):
-            src = raw[piece][:].rearrange("p j c -> p c j")
-            nc.gpsimd.tensor_scalar(unit.rearrange("p (c j) -> p c j", j=PACK), src, 1.0, 0.0, ALU.mult, ALU.add)
+            src = raw[piece][:].rearrange("p j (c i) -> p c j i", i=4)
+            dst = unit.rearrange("p (c i j) -> p c j i", i=4, j=PACK)
+            nc.gpsimd.tensor_scalar(dst, src, 1.0, 0.0, ALU.mult, ALU.add)
 
         def quantise_w1(pieces, rounded_w1):
             name = "%d%d" % pieces[0]
@@ -220,9 +221,7 @@ def tile_list_fiddle_phrase_variation_kernel(
             else:
                 cut = X0_SCALAR_CUT
                 nc.scalar.copy(dst[:, : cut // 4], src[:, : cut // 4])
-                dst = x_grouped[b][:].rearrange("p (m t) -> p m t", t=PACK)[:, cut:]
-                src = dealt[b][:].rearrange("p t m -> p m t")[:, cut:]
-                nc.gpsimd.tensor_scalar(dst, src, 1.0, 0.0, ALU.mult, ALU.add)
+                nc.gpsimd.tensor_scalar(dst[:, cut // 4 :], src[:, cut // 4 :], 1.0, 0.0, ALU.mult, ALU.add)
 
         def quantise_x(b):
             x_codes[b] = tile([P, M], U32, f"x_codes{b}")

@@ -29,15 +29,17 @@ ROWS = 4
 PER_COLUMN = 16
 SLICES = H // P
 WIDE = 256
-GROUPS = H // WIDE
-PER_GROUP = WIDE // P
+GROUP_SLICES = ((0,), (1,), (2, 3), (4, 5), (6, 7))
+GROUPS = len(GROUP_SLICES)
 UNIT = PACK * WIDE
 GPSIMD_SUMS = 5
 TENSOR_SUM = 1
 TENSOR_LAG = 4
-Y_BANKS = 4
+Y_BANKS = 6
+AHEAD = 3
 SCALAR_CUT = 176
 X0_SCALAR_CUT = 320
+RUN = 4
 
 
 def tile_list_fiddle_phrase_variation_kernel(
@@ -70,14 +72,28 @@ def tile_list_fiddle_phrase_variation_kernel(
             words = tab_words[a].rearrange("p t i -> p (t i)").bitcast(I32)
             nc.sync.dma_start(out=tab_w[a][:, cols], in_=words[:, cols])
 
+        line = tile([P, 11 * M], BF16, "line")
+
+        def place(first, count=2):
+            return line[:, first * M : (first + count) * M]
+
         raw = {}
 
         def load_w1(g, a):
-            raw[g, a] = tile([P, PACK, WIDE], F32, f"raw{g}{a}")
-            rows = w1[a * PASS : (a + 1) * PASS, g * WIDE : (g + 1) * WIDE]
-            nc.sync.dma_start(out=raw[g, a][:], in_=rows.rearrange("(p j) c -> p j c", j=PACK))
+            first, width = GROUP_SLICES[g][0] * P, len(GROUP_SLICES[g]) * P
+            if (g, a) == (GROUPS - 1, 0):
+                raw["twin"] = tile([P, PACK, 2 * width], F32, "twin")[:]
+            if g == GROUPS - 1 and a < 2:
+                raw[g, a] = raw["twin"][:, :, a * width : (a + 1) * width]
+            elif (g, a) == (2, 2):
+                raw[g, a] = place(7, PACK).bitcast(F32).rearrange("p (j c) -> p j c", j=PACK)
+            else:
+                raw[g, a] = tile([P, PACK, width], F32, f"raw{g}{a}")[:]
+            rows = w1[a * PASS : (a + 1) * PASS, first : first + width]
+            nc.sync.dma_start(out=raw[g, a], in_=rows.rearrange("(p j) c -> p j c", j=PACK))
 
         load_w1(0, 0)
+        load_w1(0, 1)
         load_table(0)
         for q in range(QUADS):
             nc.gpsimd.dma_start(
@@ -87,13 +103,14 @@ def tile_list_fiddle_phrase_variation_kernel(
         nc.sync.dma_start(offs_sb[:], offs)
         nc.sync.dma_start(pos1_sb[:], pos1)
         nc.sync.dma_start(pos2_sb[:], pos2)
-        load_w1(0, 1)
-        load_w1(0, 2)
-        load_table(1, slice(0, T // 2))
+        load_table(1, slice(0, T // 4))
+        load_table(1, slice(T // 4, T // 2))
         nc.sync.dma_start(out=staged[:SLICES, :], in_=gn.rearrange("(s p) -> s p", p=P))
         nc.sync.dma_start(out=staged[SLICES : 2 * SLICES, :], in_=rs.rearrange("(s p) -> s p", p=P))
         load_table(1, slice(T // 2, T))
-        load_table(2)
+        load_table(2, slice(0, T // 2))
+        load_w1(0, 2)
+        load_table(2, slice(T // 2, T))
         for g in range(1, GROUPS):
             for a in range(K_PASSES):
                 load_w1(g, a)
@@ -126,34 +143,31 @@ def tile_list_fiddle_phrase_variation_kernel(
         quantised = {}
 
         def round_on(copy, piece, unit):
-            src = raw[piece][:].rearrange("p j (c i) -> p c j i", i=4)
+            src = raw[piece].rearrange("p j (c i) -> p c j i", i=4)
             copy(unit.rearrange("p (c i j) -> p c j i", i=4, j=PACK), src)
 
         def round_on_scalar(piece, unit):
             round_on(nc.scalar.copy, piece, unit)
 
         def round_on_gpsimd(piece, unit):
-            src = raw[piece][:].rearrange("p j (c i) -> p c j i", i=4)
-            dst = unit.rearrange("p (c i j) -> p c j i", i=4, j=PACK)
+            src = raw[piece].rearrange("p j (c i) -> p c j i", i=RUN)
+            dst = unit.rearrange("p (c i j) -> p c j i", i=RUN, j=PACK)
             nc.gpsimd.tensor_scalar(dst, src, 1.0, 0.0, ALU.mult, ALU.add)
 
         def quantise_w1(pieces, rounded_w1):
             name = "%d%d" % pieces[0]
-            codes = tile([P, len(pieces) * WIDE], U32, f"codes{name}")
-            scales = tile([P, len(pieces) * WIDE], U8, f"scales{name}")
-            nc.vector.quantize_mx(out=codes[:].bitcast(FP8X4), scales=scales[:], in_=rounded_w1)
+            width = len(GROUP_SLICES[pieces[0][0]]) * P
+            codes = tile([P, len(pieces) * width], U32, f"codes{name}")[:]
+            scales = tile([P, len(pieces) * width], U8, f"scales{name}")
+            nc.vector.quantize_mx(out=codes.bitcast(FP8X4), scales=scales[:], in_=rounded_w1)
             for n, piece in enumerate(pieces):
-                quantised[piece] = (codes[:, n * WIDE : (n + 1) * WIDE], scales[:, n * WIDE : (n + 1) * WIDE])
-
-        line = tile([P, 13 * M], BF16, "line")
-
-        def place(first, count=2):
-            return line[:, first * M : (first + count) * M]
+                quantised[piece] = (codes[:, n * width : (n + 1) * width], scales[:, n * width : (n + 1) * width])
 
         banks = {}
 
         def first_product(s, a, half):
-            g, u = divmod(s, PER_GROUP)
+            g = [s in slices for slices in GROUP_SLICES].index(True)
+            u = GROUP_SLICES[g].index(s)
             codes, scales = quantised[g, a]
             if a == 0:
                 banks[s, half] = psum.tile([P, BANK], F32, name=f"bank{(HALVES * s + half) % 8}")
@@ -169,7 +183,7 @@ def tile_list_fiddle_phrase_variation_kernel(
             )
 
         def first_products(g, passes):
-            for s in range(PER_GROUP * g, PER_GROUP * (g + 1)):
+            for s in GROUP_SLICES[g]:
                 for a in passes:
                     for half in range(HALVES):
                         first_product(s, a, half)
@@ -177,8 +191,8 @@ def tile_list_fiddle_phrase_variation_kernel(
         h = {}
         parents = {}
 
-        def copy_h(s):
-            h[s] = tile([P, S], F32, f"h{s}")
+        def copy_h(s, tag=None):
+            h[s] = tile([P, S], F32, f"h{s}", tag)
             for half in range(HALVES):
                 dst = h[s][:, half * BANK : (half + 1) * BANK]
                 nc.scalar.copy(dst, banks[s, half][:])
@@ -187,7 +201,7 @@ def tile_list_fiddle_phrase_variation_kernel(
             parents[s] = tile([P, M], F32, f"parents{s}")[:] if room is None else room
             nc.vector.tensor_copy(parents[s], h[s][:].indirect(pos1_sb[:]))
 
-        dealt = [tile([P, PACK, M], BF16, f"dealt{b}", f"raw0{b}") for b in range(H_PASSES)]
+        dealt = [tile([P, PACK, M], BF16, f"dealt{b}", f"raw2{b}") for b in range(H_PASSES)]
         squashed = {}
 
         def squash(s, room):
@@ -211,7 +225,7 @@ def tile_list_fiddle_phrase_variation_kernel(
         x_scales = [tile([P, M], U8, f"x_scales{b}") for b in range(H_PASSES)]
 
         def interleave_x(b):
-            x_grouped[b] = tile([P, M * PACK], BF16, "x_grouped0", "raw20") if b == 0 else place(5, PACK)
+            x_grouped[b] = tile([P, M * PACK], BF16, "x_grouped0", "raw30") if b == 0 else place(5, PACK)
             dst = x_grouped[b][:].rearrange("p (c i t) -> p c t i", i=4, t=PACK)
             src = dealt[b][:].rearrange("p t (c i) -> p c t i", i=4)
             if b == H_PASSES - 1:
@@ -221,7 +235,9 @@ def tile_list_fiddle_phrase_variation_kernel(
             else:
                 cut = X0_SCALAR_CUT
                 nc.scalar.copy(dst[:, : cut // 4], src[:, : cut // 4])
-                nc.gpsimd.tensor_scalar(dst[:, cut // 4 :], src[:, cut // 4 :], 1.0, 0.0, ALU.mult, ALU.add)
+                dst = x_grouped[b][:].rearrange("p (c i t) -> p c t i", i=RUN, t=PACK)
+                src = dealt[b][:].rearrange("p t (c i) -> p c t i", i=RUN)
+                nc.gpsimd.tensor_scalar(dst[:, cut // RUN :], src[:, cut // RUN :], 1.0, 0.0, ALU.mult, ALU.add)
 
         def quantise_x(b):
             x_codes[b] = tile([P, M], U32, f"x_codes{b}")
@@ -233,72 +249,73 @@ def tile_list_fiddle_phrase_variation_kernel(
             skip[s] = room
             nc.vector.tensor_copy(room, h[s][:].indirect(pos2_sb[:]))
 
-        def fetch_half_skip(s, room, half):
-            skip[s] = room
+        def gather_half_skip(s, room, half):
             columns = M // PER_COLUMN // 2
-            nc.vector.tensor_copy(
-                room[:, half * M // 2 : (half + 1) * M // 2],
-                h[s][:].indirect(pos2_sb[:, half * columns : (half + 1) * columns]),
-            )
+            nc.vector.tensor_copy(room, h[s][:].indirect(pos2_sb[:, half * columns : (half + 1) * columns]))
 
         gather_table(0)
         nc.vector.tensor_copy(v_s[:], tab_s[:].indirect(offs_sb[:]))
+        unit = tile([P, K_PASSES * M], BF16, "unit")
         for a in range(K_PASSES):
-            unit = tile([P, UNIT], BF16, f"unit{a}")
-            round_on_scalar((0, a), unit[:])
-            quantise_w1([(0, a)], unit[:])
+            round_on_scalar((0, a), unit[:, a * M : (a + 1) * M])
+        quantise_w1([(0, a) for a in range(K_PASSES)], unit[:])
         for a in range(1, K_PASSES):
             gather_table(a)
         for a in range(K_PASSES):
             for half in range(HALVES):
-                for s in range(PER_GROUP):
-                    first_product(s, a, half)
-        round_on_gpsimd((1, 0), place(0))
-        round_on(nc.vector.tensor_copy, (1, 1), place(2))
-        copy_h(0)
+                first_product(0, a, half)
+        round_on_gpsimd((1, 0), place(0, 1))
+        round_on_scalar((1, 1), place(1, 1))
+        round_on_gpsimd((1, 2), place(2, 1))
+        copy_h(0, "raw11")
+        quantise_w1([(1, a) for a in range(K_PASSES)], place(0, 3))
+        first_products(1, range(K_PASSES))
+        round_on(nc.vector.tensor_copy, (2, 0), place(2))
+        round_on_gpsimd((2, 1), place(4))
         copy_h(1)
-        quantise_w1([(1, 0), (1, 1)], place(0, 4))
-        first_products(1, [0, 1])
         fetch_parents(0, place(0).bitcast(F32))
-        fetch_skip(0, tile([P, M], F32, "skip0", "raw11")[:])
-        round_on_scalar((1, 2), place(4))
-        round_on_gpsimd((2, 0), place(6))
-        quantise_w1([(1, 2), (2, 0)], place(4, 4))
-        first_products(1, [2])
-        first_products(2, [0])
-        fetch_parents(1, place(5).bitcast(F32))
-        fetch_half_skip(1, place(4).bitcast(F32), 0)
-        round_on_scalar((2, 1), place(9))
-        round_on_gpsimd((2, 2), place(7))
+        quantise_w1([(2, 0), (2, 1)], place(2, 4))
+        first_products(2, [0, 1])
+        fetch_parents(1, tile([P, M], F32, "parents1", "raw21")[:])
+        round_on_scalar((2, 2), place(4))
+        round_on_gpsimd((3, 0), place(2))
+        quantise_w1([(3, 0), (2, 2)], place(2, 4))
+        first_products(2, [2])
+        first_products(3, [0])
+        fetch_skip(0, place(2).bitcast(F32))
+        skip[1] = place(4).bitcast(F32)
+        gather_half_skip(1, skip[1][:, : M // 2], 0)
+        round_on_scalar((3, 1), place(7))
+        round_on_gpsimd((3, 2), place(5))
         copy_h(2)
         copy_h(3)
-        quantise_w1([(2, 2), (2, 1)], place(7, 4))
-        first_products(2, [1, 2])
-        fetch_parents(2, place(7).bitcast(F32))
-        fetch_parents(3)
-        round_on_gpsimd((3, 0), place(9))
-        round_on_gpsimd((3, 1), place(11))
+        quantise_w1([(3, 2), (3, 1)], place(5, 4))
+        first_products(3, [1, 2])
+        room23 = tile([P, 2, M], F32, "room23", "raw32")
+        fetch_parents(2, room23[:, 0, :])
+        fetch_parents(3, room23[:, 1, :])
+        round_on_gpsimd("twin", place(5, 4))
         copy_h(4)
         copy_h(5)
-        quantise_w1([(3, 0), (3, 1)], place(9, 4))
-        first_products(3, [0, 1])
-        fetch_parents(4, place(11).bitcast(F32))
-        round_on_gpsimd((3, 2), place(9))
-        quantise_w1([(3, 2)], place(9))
-        first_products(3, [2])
-        last_room = tile([P, 2, M], F32, "last_room", "raw32")
+        quantise_w1([(4, 0), (4, 1)], place(5, 4))
+        first_products(4, [0, 1])
+        middle = tile([P, 5, M], F32, "middle", "twin")
+        fetch_parents(4, middle[:, 4, :])
+        round_on_gpsimd((4, 2), place(5))
+        quantise_w1([(4, 2)], place(5))
+        first_products(4, [2])
+        last_room = tile([P, 2, M], F32, "last_room", "raw42")
         fetch_parents(5, last_room[:, 0, :])
         for s in range(6, SLICES):
             copy_h(s)
             fetch_parents(s)
-        squash(0, tile([P, M], F32, "squashed0", "raw21")[:])
-        middle = tile([P, 4, M], F32, "middle", "raw31")
-        late = tile([P, 3, M], F32, "late", "scales32")
-        rounded = tile([P, SLICES - 2, M], BF16, "rounded", "codes32")
+        squash(0, tile([P, M], F32, "squashed0", "raw31")[:])
+        late = tile([P, 3, M], F32, "late", "scales42")
+        rounded = tile([P, SLICES - 2, M], BF16, "rounded", "codes42")
         for s in range(1, SLICES):
             squash(s, middle[:, s - 1, :] if s <= 4 else late[:, s - 5, :])
         for s in range(SLICES):
-            gain_and_deal(s, place(9 + s, 1) if s < 2 else rounded[:, s - 2, :])
+            gain_and_deal(s, place(5 + s, 1) if s < 2 else rounded[:, s - 2, :])
         interleave_x(0)
         quantise_x(0)
         interleave_x(1)
@@ -309,7 +326,7 @@ def tile_list_fiddle_phrase_variation_kernel(
         rooms = [tile([P, SLICES, M], F32, f"room{a}", f"tab_w{a}") for a in range(K_PASSES)]
         sums = []
 
-        middle_sum = tile([P, M], F32, "middle_sum", "h0")
+        middle_sum = tile([P, M], F32, "middle_sum", "raw11")
 
         def add_on_tensor(res, gated, z, rows):
             there = psum.tile([P, BANK], F32, name=f"bank{Y_BANKS}")
@@ -326,12 +343,13 @@ def tile_list_fiddle_phrase_variation_kernel(
 
         for s in range(2, 6):
             fetch_skip(s, skip_room[s])
-        fetch_half_skip(1, skip[1], 1)
+        gather_half_skip(1, skip[1][:, M // 2 :], 1)
         for s in range(SLICES):
             if s >= 6:
                 fetch_skip(s, skip_room[s])
             y = psum.tile([P, BANK], F32, name=f"bank{s % Y_BANKS}")
-            for a in range(H_PASSES):
+            order = range(H_PASSES) if s < AHEAD else range(H_PASSES - 1, -1, -1)
+            for a in order:
                 col = a * H + s * P
                 nc.tensor.matmul_mx(
                     out=y[:],
@@ -339,8 +357,8 @@ def tile_list_fiddle_phrase_variation_kernel(
                     lhsT_scale=w2_s[:, col : col + P],
                     rhs=x_codes[a][:].bitcast(FP8X4),
                     rhs_scale=x_scales[a][:],
-                    start=(a == 0),
-                    stop=(a == H_PASSES - 1),
+                    start=(a == order[0]),
+                    stop=(a == order[-1]),
                 )
             z, gated, res = (room[:, s, :] for room in rooms)
             if s == TENSOR_SUM + TENSOR_LAG + 1:

from contextlib import ExitStack

import concourse.mybir as mybir
from concourse.masks import make_identity

T, S, M, K, H = 4096, 1024, 512, 1536, 1024
FLOPS = 2 * K * H * S + 2 * H * H * M

F32 = mybir.dt.float32
BF16 = mybir.dt.bfloat16
I32 = mybir.dt.int32
U32 = mybir.dt.uint32
U16 = mybir.dt.uint16
U8 = mybir.dt.uint8
FP8X4 = mybir.dt.float8_e4m3fn_x4
FP4X4 = mybir.dt.float4_e2m1fn_x4
ACT = mybir.ActivationFunctionType
ALU = mybir.AluOpType

P = 128
PACK = 4
PASS = P * PACK
K_PASSES = K // PASS
H_PASSES = H // PASS
BANK = 512
HALVES = S // BANK
QUADS = 4
ROWS = 4
PER_COLUMN = 16
SLICES = H // P
WIDE = 256
GROUP_SLICES = ((0,), (1,), (2, 3), (4, 5), (6, 7))
GROUPS = len(GROUP_SLICES)
UNIT = PACK * WIDE
GPSIMD_SUMS = 5
TENSOR_SUM = 1
TENSOR_LAG = 4
Y_BANKS = 6
AHEAD = 3
SCALAR_CUT = 176
X0_SCALAR_CUT = 320
RUN = 4


def tile_list_fiddle_phrase_variation_kernel(
    tc, tab_words, tab_scales, offs, pos1, pos2, w1, w2_words, w2_scales, gn, rs, out
):
    nc = tc.nc
    with ExitStack() as ctx:
        keep = ctx.enter_context(tc.tile_pool(name="keep", bufs=1))
        psum = ctx.enter_context(tc.psum_pool(name="psum", bufs=1))

        def tile(shape, dtype, name, tag=None):
            return keep.tile(shape, dtype, name=name, tag=tag or name, align_bytes=256)

        offs_sb = keep.tile([P, S // PER_COLUMN], U16, name="offs_sb")
        pos1_sb = keep.tile([P, M // PER_COLUMN], U16, name="pos1_sb")
        pos2_sb = keep.tile([P, M // PER_COLUMN], U16, name="pos2_sb")
        tab_w = [tile([P, T], I32, f"tab_w{a}") for a in range(K_PASSES)]
        tab_s = tile([P, T], U8, "tab_s")
        w2_w = tile([P, H_PASSES * H * 2], U8, "w2_w")
        w2_s = tile([P, H_PASSES * H], U8, "w2_s")
        staged = tile([P, P], F32, "staged")
        identity = tile([P, P], F32, "identity")
        factors = tile([P, 2 * SLICES], F32, "factors")

        nc.vector.memset(tab_s[:].bitcast(I32), 0)
        nc.vector.memset(staged[:], 0.0)
        nc.vector.memset(w2_s[:].bitcast(I32), 0)

        def load_table(a, cols=slice(0, T)):
            words = tab_words[a].rearrange("p t i -> p (t i)").bitcast(I32)
            nc.sync.dma_start(out=tab_w[a][:, cols], in_=words[:, cols])

        line = tile([P, 11 * M], BF16, "line")

        def place(first, count=2):
            return line[:, first * M : (first + count) * M]

        raw = {}

        def load_w1(g, a):
            first, width = GROUP_SLICES[g][0] * P, len(GROUP_SLICES[g]) * P
            if (g, a) == (GROUPS - 1, 0):
                raw["twin"] = tile([P, PACK, 2 * width], F32, "twin")[:]
            if g == GROUPS - 1 and a < 2:
                raw[g, a] = raw["twin"][:, :, a * width : (a + 1) * width]
            elif (g, a) == (2, 2):
                raw[g, a] = place(7, PACK).bitcast(F32).rearrange("p (j c) -> p j c", j=PACK)
            else:
                raw[g, a] = tile([P, PACK, width], F32, f"raw{g}{a}")[:]
            rows = w1[a * PASS : (a + 1) * PASS, first : first + width]
            nc.sync.dma_start(out=raw[g, a], in_=rows.rearrange("(p j) c -> p j c", j=PACK))

        load_w1(0, 0)
        load_w1(0, 1)
        load_table(0)
        for q in range(QUADS):
            nc.gpsimd.dma_start(
                out=tab_s[32 * q : 32 * q + ROWS * K_PASSES, :].bitcast(I32),
                in_=tab_scales[:, ROWS * q : ROWS * (q + 1), :].bitcast(I32),
            )
        nc.sync.dma_start(offs_sb[:], offs)
        nc.sync.dma_start(pos1_sb[:], pos1)
        nc.sync.dma_start(pos2_sb[:], pos2)
        load_table(1, slice(0, T // 4))
        load_table(1, slice(T // 4, T // 2))
        nc.sync.dma_start(out=staged[:SLICES, :], in_=gn.rearrange("(s p) -> s p", p=P))
        nc.sync.dma_start(out=staged[SLICES : 2 * SLICES, :], in_=rs.rearrange("(s p) -> s p", p=P))
        load_table(1, slice(T // 2, T))
        load_table(2, slice(0, T // 2))
        load_w1(0, 2)
        load_table(2, slice(T // 2, T))
        for g in range(1, GROUPS):
            for a in range(K_PASSES):
                load_w1(g, a)
        nc.sync.dma_start(
            out=w2_w[:].bitcast(I32).rearrange("p (a c) -> p a c", a=H_PASSES),
            in_=w2_words.bitcast(I32).rearrange("a p c -> p a c"),
        )
        for q in range(QUADS):
            nc.sync.dma_start(
                out=w2_s[32 * q : 32 * q + ROWS, :].bitcast(I32).rearrange("r (a c) -> r a c", a=H_PASSES),
                in_=w2_scales[:, ROWS * q : ROWS * (q + 1), :].bitcast(I32).rearrange("a r c -> r a c"),
            )

        make_identity(nc, identity[:])
        turned = psum.tile([P, BANK], F32, name="bank7")
        nc.tensor.transpose(turned[:, :P], staged[:], identity[:])
        nc.scalar.copy(factors[:], turned[:, : 2 * SLICES])

        v_w = [tile([P, S], U32, f"v_w{a}") for a in range(K_PASSES)]
        v_s = tile([P, S], U8, "v_s")

        def gather_table(a):
            columns = BANK // PER_COLUMN
            for half in range(HALVES):
                nc.vector.tensor_copy(
                    v_w[a][:, half * BANK : (half + 1) * BANK],
                    tab_w[a][:].bitcast(U32).indirect(offs_sb[:, half * columns : (half + 1) * columns]),
                )

        quantised = {}

        def round_on(copy, piece, unit):
            src = raw[piece].rearrange("p j (c i) -> p c j i", i=4)
            copy(unit.rearrange("p (c i j) -> p c j i", i=4, j=PACK), src)

        def round_on_scalar(piece, unit):
            round_on(nc.scalar.copy, piece, unit)

        def round_on_gpsimd(piece, unit):
            src = raw[piece].rearrange("p j (c i) -> p c j i", i=RUN)
            dst = unit.rearrange("p (c i j) -> p c j i", i=RUN, j=PACK)
            nc.gpsimd.tensor_scalar(dst, src, 1.0, 0.0, ALU.mult, ALU.add)

        def quantise_w1(pieces, rounded_w1):
            name = "%d%d" % pieces[0]
            width = len(GROUP_SLICES[pieces[0][0]]) * P
            codes = tile([P, len(pieces) * width], U32, f"codes{name}")[:]
            scales = tile([P, len(pieces) * width], U8, f"scales{name}")
            nc.vector.quantize_mx(out=codes.bitcast(FP8X4), scales=scales[:], in_=rounded_w1)
            for n, piece in enumerate(pieces):
                quantised[piece] = (codes[:, n * width : (n + 1) * width], scales[:, n * width : (n + 1) * width])

        banks = {}

        def first_product(s, a, half):
            g = [s in slices for slices in GROUP_SLICES].index(True)
            u = GROUP_SLICES[g].index(s)
            codes, scales = quantised[g, a]
            if a == 0:
                banks[s, half] = psum.tile([P, BANK], F32, name=f"bank{(HALVES * s + half) % 8}")
            cols = slice(half * BANK, (half + 1) * BANK)
            nc.tensor.matmul_mx(
                out=banks[s, half][:],
                lhsT=codes[:, u * P : (u + 1) * P].bitcast(FP8X4),
                lhsT_scale=scales[:, u * P : (u + 1) * P],
                rhs=v_w[a][:, cols].bitcast(FP8X4),
                rhs_scale=v_s[ROWS * a :, cols],
                start=(a == 0),
                stop=(a == K_PASSES - 1),
            )

        def first_products(g, passes):
            for s in GROUP_SLICES[g]:
                for a in passes:
                    for half in range(HALVES):
                        first_product(s, a, half)

        h = {}
        parents = {}

        def copy_h(s, tag=None):
            h[s] = tile([P, S], F32, f"h{s}", tag)
            for half in range(HALVES):
                dst = h[s][:, half * BANK : (half + 1) * BANK]
                nc.scalar.copy(dst, banks[s, half][:])

        def fetch_parents(s, room=None):
            parents[s] = tile([P, M], F32, f"parents{s}")[:] if room is None else room
            nc.vector.tensor_copy(parents[s], h[s][:].indirect(pos1_sb[:]))

        dealt = [tile([P, PACK, M], BF16, f"dealt{b}", f"raw2{b}") for b in range(H_PASSES)]
        squashed = {}

        def squash(s, room):
            squashed[s] = room
            nc.scalar.activation(room, parents[s], ACT.Tanh)

        def gain_and_deal(s, rounded):
            gain = factors[:, s : s + 1]
            if s == SLICES - 1:
                nc.scalar.activation(rounded, squashed[s], ACT.Copy, scale=gain)
            else:
                nc.gpsimd.tensor_scalar(rounded, squashed[s], gain, 0.0, ALU.mult, ALU.add)
            b, quad = divmod(s, QUADS)
            nc.sync.dma_start(
                out=dealt[b][32 * quad : 32 * (quad + 1)].rearrange("q t m -> q (t m)").bitcast(I32),
                in_=rounded.bitcast(I32),
            )

        x_grouped = {}
        x_codes = {}
        x_scales = [tile([P, M], U8, f"x_scales{b}") for b in range(H_PASSES)]

        def interleave_x(b):
            x_grouped[b] = tile([P, M * PACK], BF16, "x_grouped0", "raw30") if b == 0 else place(5, PACK)
            dst = x_grouped[b][:].rearrange("p (c i t) -> p c t i", i=4, t=PACK)
            src = dealt[b][:].rearrange("p t (c i) -> p c t i", i=4)
            if b == H_PASSES - 1:
                cut = SCALAR_CUT // 4
                nc.scalar.copy(dst[:, :cut], src[:, :cut])
                nc.vector.tensor_copy(dst[:, cut:], src[:, cut:])
            else:
                cut = X0_SCALAR_CUT
                nc.scalar.copy(dst[:, : cut // 4], src[:, : cut // 4])
                dst = x_grouped[b][:].rearrange("p (c i t) -> p c t i", i=RUN, t=PACK)
                src = dealt[b][:].rearrange("p t (c i) -> p c t i", i=RUN)
                nc.gpsimd.tensor_scalar(dst[:, cut // RUN :], src[:, cut // RUN :], 1.0, 0.0, ALU.mult, ALU.add)

        def quantise_x(b):
            x_codes[b] = tile([P, M], U32, f"x_codes{b}")
            nc.vector.quantize_mx(out=x_codes[b][:].bitcast(FP8X4), scales=x_scales[b][:], in_=x_grouped[b][:])

        skip = {}

        def fetch_skip(s, room):
            skip[s] = room
            nc.vector.tensor_copy(room, h[s][:].indirect(pos2_sb[:]))

        def gather_half_skip(s, room, half):
            columns = M // PER_COLUMN // 2
            nc.vector.tensor_copy(room, h[s][:].indirect(pos2_sb[:, half * columns : (half + 1) * columns]))

        gather_table(0)
        nc.vector.tensor_copy(v_s[:], tab_s[:].indirect(offs_sb[:]))
        unit = tile([P, K_PASSES * M], BF16, "unit")
        for a in range(K_PASSES):
            round_on_scalar((0, a), unit[:, a * M : (a + 1) * M])
        quantise_w1([(0, a) for a in range(K_PASSES)], unit[:])
        for a in range(1, K_PASSES):
            gather_table(a)
        for a in range(K_PASSES):
            for half in range(HALVES):
                first_product(0, a, half)
        round_on_gpsimd((1, 0), place(0, 1))
        round_on_scalar((1, 1), place(1, 1))
        round_on_gpsimd((1, 2), place(2, 1))
        copy_h(0, "raw11")
        quantise_w1([(1, a) for a in range(K_PASSES)], place(0, 3))
        first_products(1, range(K_PASSES))
        round_on(nc.vector.tensor_copy, (2, 0), place(2))
        round_on_gpsimd((2, 1), place(4))
        copy_h(1)
        fetch_parents(0, place(0).bitcast(F32))
        quantise_w1([(2, 0), (2, 1)], place(2, 4))
        first_products(2, [0, 1])
        fetch_parents(1, tile([P, M], F32, "parents1", "raw21")[:])
        round_on_scalar((2, 2), place(4))
        round_on_gpsimd((3, 0), place(2))
        quantise_w1([(3, 0), (2, 2)], place(2, 4))
        first_products(2, [2])
        first_products(3, [0])
        fetch_skip(0, place(2).bitcast(F32))
        skip[1] = place(4).bitcast(F32)
        gather_half_skip(1, skip[1][:, : M // 2], 0)
        round_on_scalar((3, 1), place(7))
        round_on_gpsimd((3, 2), place(5))
        copy_h(2)
        copy_h(3)
        quantise_w1([(3, 2), (3, 1)], place(5, 4))
        first_products(3, [1, 2])
        room23 = tile([P, 2, M], F32, "room23", "raw32")
        fetch_parents(2, room23[:, 0, :])
        fetch_parents(3, room23[:, 1, :])
        round_on_gpsimd("twin", place(5, 4))
        copy_h(4)
        copy_h(5)
        quantise_w1([(4, 0), (4, 1)], place(5, 4))
        first_products(4, [0, 1])
        middle = tile([P, 5, M], F32, "middle", "twin")
        fetch_parents(4, middle[:, 4, :])
        round_on_gpsimd((4, 2), place(5))
        quantise_w1([(4, 2)], place(5))
        first_products(4, [2])
        last_room = tile([P, 2, M], F32, "last_room", "raw42")
        fetch_parents(5, last_room[:, 0, :])
        for s in range(6, SLICES):
            copy_h(s)
            fetch_parents(s)
        squash(0, tile([P, M], F32, "squashed0", "raw31")[:])
        late = tile([P, 3, M], F32, "late", "scales42")
        rounded = tile([P, SLICES - 2, M], BF16, "rounded", "codes42")
        for s in range(1, SLICES):
            squash(s, middle[:, s - 1, :] if s <= 4 else late[:, s - 5, :])
        for s in range(SLICES):
            gain_and_deal(s, place(5 + s, 1) if s < 2 else rounded[:, s - 2, :])
        interleave_x(0)
        quantise_x(0)
        interleave_x(1)
        quantise_x(1)

        skip_room = [skip[0], skip[1], last_room[:, 1, :], parents[5], parents[6], parents[7]]
        skip_room = skip_room + skip_room[4:6]
        rooms = [tile([P, SLICES, M], F32, f"room{a}", f"tab_w{a}") for a in range(K_PASSES)]
        sums = []

        middle_sum = tile([P, M], F32, "middle_sum", "raw11")

        def add_on_tensor(res, gated, z, rows):
            there = psum.tile([P, BANK], F32, name=f"bank{Y_BANKS}")
            back = psum.tile([P, BANK], F32, name=f"bank{Y_BANKS + 1}")
            for c in range(0, M, P):
                cols = slice(c, c + P)
                nc.tensor.matmul(there[:, cols], z[:, cols], identity[:], start=True, stop=False, is_transpose=True)
                nc.tensor.matmul(there[:, cols], gated[:, cols], identity[:], start=False, stop=True, is_transpose=True)
            nc.scalar.copy(middle_sum[:], there[:])
            for c in range(0, M, P):
                nc.tensor.transpose(back[:, c : c + P], middle_sum[:, c : c + P], identity[:])
            nc.scalar.copy(res, back[:])
            nc.sync.dma_start(out=rows, in_=res)

        for s in range(2, 6):
            fetch_skip(s, skip_room[s])
        gather_half_skip(1, skip[1][:, M // 2 :], 1)
        for s in range(SLICES):
            if s >= 6:
                fetch_skip(s, skip_room[s])
            y = psum.tile([P, BANK], F32, name=f"bank{s % Y_BANKS}")
            order = range(H_PASSES) if s < AHEAD else range(H_PASSES - 1, -1, -1)
            for a in order:
                col = a * H + s * P
                nc.tensor.matmul_mx(
                    out=y[:],
                    lhsT=w2_w[:, 2 * col : 2 * (col + P)].bitcast(FP4X4),
                    lhsT_scale=w2_s[:, col : col + P],
                    rhs=x_codes[a][:].bitcast(FP8X4),
                    rhs_scale=x_scales[a][:],
                    start=(a == order[0]),
                    stop=(a == order[-1]),
                )
            z, gated, res = (room[:, s, :] for room in rooms)
            if s == TENSOR_SUM + TENSOR_LAG + 1:
                gated = middle_sum[:]
            adder = nc.gpsimd if s < GPSIMD_SUMS else nc.vector
            width = M // 2 if s == SLICES - 1 else M
            parts = [slice(c, c + width) for c in range(0, M, width)]
            weight = factors[:, SLICES + s : SLICES + s + 1]
            for cols in parts:
                nc.vector.scalar_tensor_tensor(z[:, cols], skip[s][:, cols], weight, y[:, cols], ALU.mult, ALU.add)
                nc.scalar.activation(gated[:, cols], z[:, cols], ACT.Silu)
            if s == TENSOR_SUM:
                turned_sum = (res, gated, z)
                continue
            if s == TENSOR_SUM + TENSOR_LAG:
                add_on_tensor(*turned_sum, out[TENSOR_SUM * P : (TENSOR_SUM + 1) * P, :])
            for cols in parts:
                sums.append((adder, res[:, cols], gated[:, cols], z[:, cols], out[s * P : (s + 1) * P, cols]))
        for adder, res, gated, z, rows in sums:
            adder.tensor_tensor(res, gated, z, ALU.add)
            nc.sync.dma_start(out=rows, in_=res)
